import numpy as np
import ml_dtypes


def mxq(x, axis, fmt="e4m3"):
    dtype, down = {"e4m3": (ml_dtypes.float8_e4m3fn, 7), "e5m2": (ml_dtypes.float8_e5m2, 14)}[fmt]
    v = np.moveaxis(np.asarray(x, np.float32).astype(ml_dtypes.bfloat16).astype(np.float64), axis, -1)
    blocks = v.reshape(v.shape[:-1] + (-1, 32))
    amax = np.abs(blocks).max(-1, keepdims=True)
    byte = np.maximum(np.where(amax > 0, np.frexp(amax)[1] - 1 + 127, 0) - down, 1)
    scale = np.exp2(byte - 127.0)
    codes = (blocks / scale).astype(np.float32).astype(dtype).astype(np.float64)
    return np.moveaxis((codes * scale).reshape(v.shape), -1, axis)


WIDE = False


def mx_kscale(k):
    if not WIDE:
        return np.ones(k)
    levels = np.array([10, -10, 5, -5, 0])
    if k % 512:
        return np.exp2(np.random.permutation(np.resize(levels, k // 32))).repeat(32)
    a = np.empty((k // 512, 16))
    for p in range(k // 512):
        a[p, :8] = np.random.permutation(np.resize(levels, 8))
        for g in range(8):
            far = levels[np.abs(levels - a[p, g]) >= 10]
            a[p, g + 8] = far[np.random.randint(len(far))]
    return np.exp2(a.ravel()).repeat(32)


def f64(x):
    return np.asarray(x).astype(np.float64)


def striped(idx):
    return np.tile(np.asarray(idx).reshape(-1, 16).T, (8, 1)).astype(np.uint16)


def unstriped(offs):
    return offs[:16].T.reshape(-1).astype(np.int64)


E2M1 = np.array([0.0, 0.5, 1.0, 1.5, 2.0, 3.0, 4.0, 6.0, -0.0, -0.5, -1.0, -1.5, -2.0, -3.0, -4.0, -6.0])


def pack_weight(w, fmt):
    k, n = w.shape
    w = f64(np.asarray(w, np.float32).astype(ml_dtypes.bfloat16)).reshape(k // 32, 32, n)
    amax = np.abs(w).max(1)
    if fmt == "e4m3":
        byte = np.frexp(amax)[1] - 1 + 127 - 7
    else:
        mant, ex = np.frexp(amax / 6.0)
        byte = np.where(mant > 0.5, ex, ex - 1) + 127
    byte = np.clip(np.where(amax > 0, byte, 1), 1, 254)
    scaled = (w * np.exp2(127.0 - byte)[:, None, :]).reshape(k, n).astype(np.float32)
    by_word = np.ascontiguousarray(scaled.reshape(k // 512, 128, 4, n).transpose(0, 1, 3, 2))
    if fmt == "e4m3":
        words = by_word.astype(ml_dtypes.float8_e4m3fn).view(np.uint8)
    else:
        c = by_word.astype(ml_dtypes.float4_e2m1fn).view(np.uint8) & 0xF
        words = (c[..., 0::2] | (c[..., 1::2] << 4)).reshape(k // 512, 128, 2 * n)
    return np.ascontiguousarray(words), np.ascontiguousarray(byte.astype(np.uint8).reshape(k // 512, 16, n))


def unpack_weight(words, scales, fmt):
    g, _, n = scales.shape
    words = np.ascontiguousarray(words).reshape(g, 128, n, -1)
    if fmt == "e4m3":
        vals = words.view(ml_dtypes.float8_e4m3fn).astype(np.float64)
    else:
        nib = np.empty((g, 128, n, 4), np.uint8)
        nib[..., 0::2] = words & 0xF
        nib[..., 1::2] = words >> 4
        vals = E2M1[nib]
    vals = vals * np.repeat(np.exp2(scales.astype(np.float64) - 127.0), 8, axis=1)[..., None]
    return vals.transpose(0, 1, 3, 2).reshape(g * 512, n)


def silu(v):
    return v / (1.0 + np.exp(-v))


B, N, T, D, NQ = 1, 512, 2048, 1024, 512


def setup_inputs():
    n = np.random.standard_normal
    pages = np.random.permutation(T // 64)[:B * N // 64]
    idx = (pages[:, None] * 64 + np.arange(64)[None, :]).reshape(-1)
    s = mx_kscale(D)[:, None]
    kp = pack_weight(n((D, T)) / s, "e2m1")
    return {
        "qT": (n((B, D, NQ)) * s * (1.00 / np.sqrt(D))).astype(np.float32),
        "k_words": np.ascontiguousarray(kp[0].reshape(1, 2, 128, T, 2).transpose(0, 2, 3, 1, 4)).reshape(1, 128, T, 4),
        "k_scales": kp[1],
        "nb": np.tile(0.5 * n(2048), (128, 1)).astype(np.float32),
        "ns": np.tile(np.random.uniform(0.2, 2.0, 2048), (128, 1)).astype(np.float32),
        "offs": striped(idx),
    }


def reference(qT, k_words, k_scales, nb, ns, offs):
    idx = unstriped(offs)
    pick = lambda x, which: x[:, which].reshape(x.shape[0], B, -1).transpose(1, 0, 2)
    k = unpack_weight(k_words.reshape(1, 128, T, 2, 2).transpose(0, 3, 1, 2, 4).reshape(2, 128, 2 * T), k_scales, "e2m1")
    kg = pick(k, idx)
    qq = mxq(f64(qT), 1, "e4m3")
    a = kg.transpose(0, 2, 1) @ qq
    y = silu(a + pick(f64(nb), idx)[:, :1, :].transpose(0, 2, 1)) * pick(f64(ns), idx)[:, :1, :].transpose(0, 2, 1)
    return y

@@ -1,0 +1,152 @@
+from contextlib import ExitStack
+
+import concourse.mybir as mybir
+from concourse.masks import make_identity
+
+N, T, D, NQ = 512, 2048, 1024, 512
+FLOPS = 2 * N * D * NQ
+
+F32 = mybir.dt.float32
+BF16 = mybir.dt.bfloat16
+I32 = mybir.dt.int32
+U32 = mybir.dt.uint32
+U16 = mybir.dt.uint16
+U8 = mybir.dt.uint8
+FP8X4 = mybir.dt.float8_e4m3fn_x4
+FP4X4 = mybir.dt.float4_e2m1fn_x4
+SILU = mybir.ActivationFunctionType.Silu
+
+P = 128
+PACK = 4
+K_PASS = P * PACK
+PASSES = D // K_PASS
+SLOT_TILES = N // P
+N_MM = 128
+ROW = P - 1
+CHUNKS = (256, 128, 128)
+VECTOR_CASTS = {(2, 0), (2, 1)}
+STORE_TILES = 2
+
+
+def tile_attend_neut_silu_kernel(tc, qT, k_words, k_scales, nb, ns, offs, out):
+    nc = tc.nc
+    starts = [sum(CHUNKS[:c]) for c in range(len(CHUNKS))]
+
+    with ExitStack() as ctx:
+        keep = ctx.enter_context(tc.tile_pool(name="keep", bufs=1))
+        turn = ctx.enter_context(tc.psum_pool(name="turn", bufs=1))
+        psum = ctx.enter_context(tc.psum_pool(name="psum", bufs=6))
+
+        offsets = keep.tile([P, N // 16], U16, name="offsets")
+        word_pool = keep.tile([P, T], I32, name="word_pool")
+        scale_pool = keep.tile([P, T], U8, name="scale_pool")
+        nb_pool = keep.tile([P, T], F32, name="nb_pool")
+        ns_pool = keep.tile([P, T], F32, name="ns_pool")
+        ident = keep.tile([P, P], F32, name="ident")
+        k_scale0 = keep.tile([P, N], U8, name="k_scale0", align_bytes=64)
+        k_scale1 = keep.tile([P, N], U8, name="k_scale1", align_bytes=64)
+        k_scale = [k_scale0, k_scale1]
+
+        raw = {}
+
+        def load_q(c, g):
+            raw[c, g] = keep.tile([P, PACK, CHUNKS[c]], F32, name=f"raw{c}_{g}")
+            rows = qT[0, g * K_PASS : (g + 1) * K_PASS, starts[c] : starts[c] + CHUNKS[c]]
+            nc.sync.dma_start(out=raw[c, g][:], in_=rows.rearrange("(p j) w -> p j w", j=PACK))
+
+        nc.vector.memset(scale_pool[:].bitcast(I32), 0)
+        nc.vector.memset(nb_pool[0:ROW, :], 0.0)
+        nc.vector.memset(ns_pool[0:ROW, :], 0.0)
+        nc.vector.memset(k_scale1[:].bitcast(I32), 0)
+        make_identity(nc, ident[:])
+
+        nc.sync.dma_start(offsets[:], offs)
+        nc.sync.dma_start(out=nb_pool[ROW : ROW + 1, :], in_=nb[0:1, :])
+        load_q(0, 0)
+        for quad in range(4):
+            nc.sync.dma_start(
+                out=scale_pool[32 * quad : 32 * quad + 8, :].bitcast(I32),
+                in_=k_scales[:, 4 * quad : 4 * quad + 4, :].bitcast(I32),
+            )
+        nc.sync.dma_start(out=ns_pool[ROW : ROW + 1, :], in_=ns[0:1, :])
+        nc.sync.dma_start(out=word_pool[:], in_=k_words[0].rearrange("p t b -> p (t b)").bitcast(I32))
+        load_q(0, 1)
+        load_q(1, 0)
+        load_q(1, 1)
+        load_q(2, 0)
+        load_q(2, 1)
+
+        nc.vector.tensor_copy(k_scale0[:], scale_pool[:].indirect(offsets[:]))
+        nc.scalar.dma_start(out=k_scale1[0:112, :].bitcast(I32), in_=k_scale0[4:116, :].bitcast(I32))
+
+        def per_partition(pool, name):
+            listed = keep.tile([P, N], F32, name=name + "_listed")
+            nc.vector.tensor_copy(listed[:], pool[:].indirect(offsets[:]))
+            turned = turn.tile([P, SLOT_TILES, P], F32, name=name + "_turned")
+            for j in range(SLOT_TILES):
+                nc.tensor.transpose(turned[:, j, :], listed[:, j * P : (j + 1) * P], ident[:])
+            cols = keep.tile([P, SLOT_TILES], F32, name=name + "_cols")
+            nc.scalar.copy(cols[:], turned[:, :, ROW])
+            return cols
+
+        grouped = {}
+
+        def cast_q(c, g):
+            grouped[c, g] = keep.tile([P, CHUNKS[c], PACK], BF16, name=f"grouped{c}_{g}", align_bytes=64)
+            dst = grouped[c, g][:].rearrange("p (c i) t -> p c t i", i=4)
+            src = raw[c, g][:].rearrange("p t (c i) -> p c t i", i=4)
+            if (c, g) in VECTOR_CASTS:
+                nc.vector.tensor_copy(dst, src)
+            else:
+                nc.scalar.copy(dst, src)
+
+        q_codes, q_scales = {}, {}
+
+        def quantize_q(c, g):
+            q_codes[c, g] = keep.tile([P, CHUNKS[c]], U32, name=f"q_codes{c}_{g}", align_bytes=64)
+            q_scales[c, g] = keep.tile([P, CHUNKS[c]], U8, name=f"q_scales{c}_{g}", align_bytes=64)
+            nc.vector.quantize_mx(
+                out=q_codes[c, g][:].bitcast(FP8X4),
+                scales=q_scales[c, g][:],
+                in_=grouped[c, g][:].rearrange("p w j -> p (w j)"),
+            )
+
+        cast_q(0, 0)
+        nb_cols = per_partition(nb_pool, "nb")
+        pairs = keep.tile([P, N], U32, name="pairs")
+        nc.vector.tensor_copy(pairs[:], word_pool[:].bitcast(U32).indirect(offsets[:]))
+        k_codes = keep.tile([P, PASSES, 2 * N], U8, name="k_codes", align_bytes=64)
+        nc.vector.tensor_copy(
+            k_codes[:].bitcast(U16), pairs[:].bitcast(U16).rearrange("p (s h) -> p h s", h=PASSES)
+        )
+        ns_cols = per_partition(ns_pool, "ns")
+
+        for c in range(len(CHUNKS)):
+            for g in range(PASSES):
+                if (c, g) != (0, 0):
+                    cast_q(c, g)
+                quantize_q(c, g)
+
+        for c in range(len(CHUNKS)):
+            width = CHUNKS[c]
+            for j0 in range(0, SLOT_TILES, STORE_TILES):
+                result = keep.tile([P, STORE_TILES, width], F32, name=f"result{c}_{j0}")
+                for j in range(j0, j0 + STORE_TILES):
+                    acc = psum.tile([P, width], F32, name="acc")
+                    for n0 in range(0, width, N_MM):
+                        cols = slice(n0, n0 + N_MM)
+                        for g in range(PASSES):
+                            nc.tensor.matmul_mx(
+                                out=acc[:, cols],
+                                lhsT=k_codes[:, g, 2 * P * j : 2 * P * (j + 1)].bitcast(FP4X4),
+                                lhsT_scale=k_scale[g][:, P * j : P * (j + 1)],
+                                rhs=q_codes[c, g][:, cols].bitcast(FP8X4),
+                                rhs_scale=q_scales[c, g][:, cols],
+                                start=(g == 0),
+                                stop=(g == PASSES - 1),
+                            )
+                    act = keep.tile([P, width], F32, name=f"act{c}_{j}")
+                    nc.scalar.activation(act[:], acc[:], SILU, bias=nb_cols[:, j : j + 1])
+                    nc.vector.tensor_scalar_mul(result[:, j - j0, :], act[:], ns_cols[:, j : j + 1])
+                rows = out[0, j0 * P : (j0 + STORE_TILES) * P, starts[c] : starts[c] + width]
+                nc.sync.dma_start(out=rows.rearrange("(j p) w -> p j w", p=P), in_=result[:])

@@ -15,6 +15,7 @@ U8 = mybir.dt.uint8
 FP8X4 = mybir.dt.float8_e4m3fn_x4
 FP4X4 = mybir.dt.float4_e2m1fn_x4
 SILU = mybir.ActivationFunctionType.Silu
+COPY = mybir.ActivationFunctionType.Copy
 
 P = 128
 PACK = 4
@@ -23,22 +24,19 @@ PASSES = D // K_PASS
 SLOT_TILES = N // P
 N_MM = 128
 ROW = P - 1
-CHUNKS = (256, 128, 128)
-VECTOR_CASTS = {(2, 0), (2, 1)}
-STORE_TILES = 2
+SHIFT = 16
+BANK = 512
 
 
 def tile_attend_neut_silu_kernel(tc, qT, k_words, k_scales, nb, ns, offs, out):
     nc = tc.nc
-    starts = [sum(CHUNKS[:c]) for c in range(len(CHUNKS))]
 
     with ExitStack() as ctx:
         keep = ctx.enter_context(tc.tile_pool(name="keep", bufs=1))
-        turn = ctx.enter_context(tc.psum_pool(name="turn", bufs=1))
-        psum = ctx.enter_context(tc.psum_pool(name="psum", bufs=6))
+        psum = ctx.enter_context(tc.psum_pool(name="psum", bufs=1))
 
         offsets = keep.tile([P, N // 16], U16, name="offsets")
-        word_pool = keep.tile([P, T], I32, name="word_pool")
+        word_pool = keep.tile([P, T], I32, name="word_pool", align_bytes=64)
         scale_pool = keep.tile([P, T], U8, name="scale_pool")
         nb_pool = keep.tile([P, T], F32, name="nb_pool")
         ns_pool = keep.tile([P, T], F32, name="ns_pool")
@@ -47,106 +45,146 @@ def tile_attend_neut_silu_kernel(tc, qT, k_words, k_scales, nb, ns, offs, out):
         k_scale1 = keep.tile([P, N], U8, name="k_scale1", align_bytes=64)
         k_scale = [k_scale0, k_scale1]
 
-        raw = {}
+        raw, grouped, q_codes, q_scales = {}, {}, {}, {}
 
-        def load_q(c, g):
-            raw[c, g] = keep.tile([P, PACK, CHUNKS[c]], F32, name=f"raw{c}_{g}")
-            rows = qT[0, g * K_PASS : (g + 1) * K_PASS, starts[c] : starts[c] + CHUNKS[c]]
-            nc.sync.dma_start(out=raw[c, g][:], in_=rows.rearrange("(p j) w -> p j w", j=PACK))
+        def load_q(g, q0, width):
+            raw[g, q0] = keep.tile([P, PACK, width], F32, name=f"raw{g}_{q0}")
+            rows = qT[0, g * K_PASS : (g + 1) * K_PASS, q0 : q0 + width]
+            nc.sync.dma_start(out=raw[g, q0][:], in_=rows.rearrange("(p j) w -> p j w", j=PACK))
 
+        def cast_q(g, q0, width, on_vector=False, first=False):
+            grouped[g, q0] = keep.tile([P, width, PACK], BF16, name=f"grouped{g}_{q0}", align_bytes=64)
+            dst = grouped[g, q0][:].rearrange("p (c i) t -> p c t i", i=4)
+            src = raw[g, q0][:].rearrange("p t (c i) -> p c t i", i=4)
+            if on_vector:
+                nc.vector.tensor_copy(dst, src)
+            elif first:
+                nc.scalar.activation(dst, src, COPY)
+            else:
+                nc.scalar.copy(dst, src)
+
+        def quantize_q(g, q0, width, tag=None):
+            codes = keep.tile([P, width], U32, name=f"q_codes{g}_{q0}", align_bytes=64, tag=tag or f"q_codes{g}_{q0}")
+            scales = keep.tile([P, width], U8, name=f"q_scales{g}_{q0}", align_bytes=64)
+            nc.vector.quantize_mx(
+                out=codes[:].bitcast(FP8X4),
+                scales=scales[:],
+                in_=grouped[g, q0][:].rearrange("p w j -> p (w j)"),
+            )
+            for n0 in range(0, width, N_MM):
+                q_codes[g, q0 + n0] = codes[:, n0 : n0 + N_MM]
+                q_scales[g, q0 + n0] = scales[:, n0 : n0 + N_MM]
+
+        ns_head = keep.tile([P, 8], F32, name="ns_head")
+        nc.scalar.dma_start(out=ns_head[:], in_=ns[:, 0:8])
+        nc.scalar.dma_start(out=nb_pool[ROW : ROW + 1, :], in_=nb[0:1, :])
+        nc.scalar.dma_start(out=ns_pool[ROW : ROW + 1, :], in_=ns[0:1, :])
+        warm = keep.tile([P, 1], F32, name="warm")
+        warm_out = keep.tile([P, 1], F32, name="warm_out")
+        nc.vector.memset(warm[:], 0.0)
+        nc.scalar.activation(warm_out[:], warm[:], SILU)
         nc.vector.memset(scale_pool[:].bitcast(I32), 0)
         nc.vector.memset(nb_pool[0:ROW, :], 0.0)
-        nc.vector.memset(ns_pool[0:ROW, :], 0.0)
         nc.vector.memset(k_scale1[:].bitcast(I32), 0)
         make_identity(nc, ident[:])
 
         nc.sync.dma_start(offsets[:], offs)
-        nc.sync.dma_start(out=nb_pool[ROW : ROW + 1, :], in_=nb[0:1, :])
-        load_q(0, 0)
-        for quad in range(4):
-            nc.sync.dma_start(
-                out=scale_pool[32 * quad : 32 * quad + 8, :].bitcast(I32),
-                in_=k_scales[:, 4 * quad : 4 * quad + 4, :].bitcast(I32),
-            )
-        nc.sync.dma_start(out=ns_pool[ROW : ROW + 1, :], in_=ns[0:1, :])
+        load_q(0, 0, 256)
+        scale_rows = k_scales.rearrange("o (a r) t -> r a o t", r=4)
+        for r in range(4):
+            nc.sync.dma_start(out=scale_pool[r:P:SHIFT, :].bitcast(I32), in_=scale_rows[r].bitcast(I32))
         nc.sync.dma_start(out=word_pool[:], in_=k_words[0].rearrange("p t b -> p (t b)").bitcast(I32))
-        load_q(0, 1)
-        load_q(1, 0)
-        load_q(1, 1)
-        load_q(2, 0)
-        load_q(2, 1)
+        load_q(1, 0, 256)
+        load_q(0, 256, 256)
+        load_q(1, 256, 128)
+        load_q(1, 384, 128)
 
+        nc.scalar.copy(
+            ns_pool[0:ROW, :].rearrange("p (a b) -> p a b", b=8),
+            ns_head[0:ROW, :].unsqueeze(1).to_broadcast([ROW, T // 8, 8]),
+        )
+        cast_q(0, 0, 256, first=False)
         nc.vector.tensor_copy(k_scale0[:], scale_pool[:].indirect(offsets[:]))
-        nc.scalar.dma_start(out=k_scale1[0:112, :].bitcast(I32), in_=k_scale0[4:116, :].bitcast(I32))
+        nc.scalar.dma_start(out=k_scale1[0 : P - SHIFT, :].bitcast(I32), in_=k_scale0[SHIFT:P, :].bitcast(I32))
 
-        def per_partition(pool, name):
+        def gather_row(pool, name):
             listed = keep.tile([P, N], F32, name=name + "_listed")
             nc.vector.tensor_copy(listed[:], pool[:].indirect(offsets[:]))
-            turned = turn.tile([P, SLOT_TILES, P], F32, name=name + "_turned")
+            return listed
+
+        def per_partition(listed, name, bank, tag):
+            turned = psum.tile([P, SLOT_TILES, P], F32, name=name + "_turned", tag=bank)
             for j in range(SLOT_TILES):
                 nc.tensor.transpose(turned[:, j, :], listed[:, j * P : (j + 1) * P], ident[:])
-            cols = keep.tile([P, SLOT_TILES], F32, name=name + "_cols")
+            cols = keep.tile([P, SLOT_TILES], F32, name=name + "_cols", tag=tag)
             nc.scalar.copy(cols[:], turned[:, :, ROW])
             return cols
 
-        grouped = {}
-
-        def cast_q(c, g):
-            grouped[c, g] = keep.tile([P, CHUNKS[c], PACK], BF16, name=f"grouped{c}_{g}", align_bytes=64)
-            dst = grouped[c, g][:].rearrange("p (c i) t -> p c t i", i=4)
-            src = raw[c, g][:].rearrange("p t (c i) -> p c t i", i=4)
-            if (c, g) in VECTOR_CASTS:
-                nc.vector.tensor_copy(dst, src)
-            else:
-                nc.scalar.copy(dst, src)
-
-        q_codes, q_scales = {}, {}
-
-        def quantize_q(c, g):
-            q_codes[c, g] = keep.tile([P, CHUNKS[c]], U32, name=f"q_codes{c}_{g}", align_bytes=64)
-            q_scales[c, g] = keep.tile([P, CHUNKS[c]], U8, name=f"q_scales{c}_{g}", align_bytes=64)
-            nc.vector.quantize_mx(
-                out=q_codes[c, g][:].bitcast(FP8X4),
-                scales=q_scales[c, g][:],
-                in_=grouped[c, g][:].rearrange("p w j -> p (w j)"),
-            )
-
-        cast_q(0, 0)
-        nb_cols = per_partition(nb_pool, "nb")
-        pairs = keep.tile([P, N], U32, name="pairs")
+        nb_cols = per_partition(gather_row(nb_pool, "nb"), "nb", "bank4", "nb_cols")
+        ns_listed = gather_row(ns_pool, "ns")
+        pairs = keep.tile([P, N], U32, name="pairs", tag="ns_pool")
         nc.vector.tensor_copy(pairs[:], word_pool[:].bitcast(U32).indirect(offsets[:]))
         k_codes = keep.tile([P, PASSES, 2 * N], U8, name="k_codes", align_bytes=64)
         nc.vector.tensor_copy(
             k_codes[:].bitcast(U16), pairs[:].bitcast(U16).rearrange("p (s h) -> p h s", h=PASSES)
         )
-        ns_cols = per_partition(ns_pool, "ns")
+        quantize_q(0, 0, 256, tag="word_pool")
 
-        for c in range(len(CHUNKS)):
-            for g in range(PASSES):
-                if (c, g) != (0, 0):
-                    cast_q(c, g)
-                quantize_q(c, g)
+        def multiply(acc, tiles, q0, width, g):
+            sums = [(i, j, n0) for i, j in enumerate(tiles) for n0 in range(0, width, N_MM)]
+            for s, (i, j, n0) in enumerate(sums):
+                nc.tensor.matmul_mx(
+                    out=acc[:, i, n0 : n0 + N_MM],
+                    lhsT=k_codes[:, g, 2 * P * j : 2 * P * (j + 1)].bitcast(FP4X4),
+                    lhsT_scale=k_scale[g][:, P * j : P * (j + 1)],
+                    rhs=q_codes[g, q0 + n0].bitcast(FP8X4),
+                    rhs_scale=q_scales[g, q0 + n0],
+                    start=(g == 0 and s == 0),
+                    stop=(g == PASSES - 1 and s == len(sums) - 1),
+                )
 
-        for c in range(len(CHUNKS)):
-            width = CHUNKS[c]
-            for j0 in range(0, SLOT_TILES, STORE_TILES):
-                result = keep.tile([P, STORE_TILES, width], F32, name=f"result{c}_{j0}")
-                for j in range(j0, j0 + STORE_TILES):
-                    acc = psum.tile([P, width], F32, name="acc")
-                    for n0 in range(0, width, N_MM):
-                        cols = slice(n0, n0 + N_MM)
-                        for g in range(PASSES):
-                            nc.tensor.matmul_mx(
-                                out=acc[:, cols],
-                                lhsT=k_codes[:, g, 2 * P * j : 2 * P * (j + 1)].bitcast(FP4X4),
-                                lhsT_scale=k_scale[g][:, P * j : P * (j + 1)],
-                                rhs=q_codes[c, g][:, cols].bitcast(FP8X4),
-                                rhs_scale=q_scales[c, g][:, cols],
-                                start=(g == 0),
-                                stop=(g == PASSES - 1),
-                            )
-                    act = keep.tile([P, width], F32, name=f"act{c}_{j}")
-                    nc.scalar.activation(act[:], acc[:], SILU, bias=nb_cols[:, j : j + 1])
-                    nc.vector.tensor_scalar_mul(result[:, j - j0, :], act[:], ns_cols[:, j : j + 1])
-                rows = out[0, j0 * P : (j0 + STORE_TILES) * P, starts[c] : starts[c] + width]
-                nc.sync.dma_start(out=rows.rearrange("(j p) w -> p j w", p=P), in_=result[:])
+        def finish(acc, tiles, q0, width, result):
+            for i, j in enumerate(tiles):
+                act = keep.tile([P, width], F32, name=f"act{q0}_{j}")
+                nc.scalar.activation(act[:], acc[:, i, :], SILU, bias=nb_cols[:, j : j + 1])
+                nc.vector.tensor_scalar_mul(result[:, i, :], act[:], ns_cols[:, j : j + 1])
+
+        def store(result, j0, count, q0, width):
+            rows = out[0, j0 * P : (j0 + count) * P, q0 : q0 + width]
+            nc.sync.dma_start(out=rows.rearrange("(j p) w -> p j w", p=P), in_=result[:])
+
+        acc_a = [psum.tile([P, 1, 256], F32, name=f"acc_a{j}", tag=f"bank{j}") for j in range(SLOT_TILES)]
+        for j in range(SLOT_TILES):
+            multiply(acc_a[j], [j], 0, 256, 0)
+
+        cast_q(1, 0, 256)
+        cast_q(0, 256, 256)
+        ns_cols = per_partition(ns_listed, "ns", "bank5", "raw0_256")
+        quantize_q(1, 0, 256)
+        for j in range(SLOT_TILES):
+            multiply(acc_a[j], [j], 0, 256, 1)
+
+        cast_q(1, 256, 128, on_vector=True)
+        quantize_q(1, 256, 128)
+        quantize_q(0, 256, 256)
+        cast_q(1, 384, 128, on_vector=True)
+        quantize_q(1, 384, 128)
+
+        late = {}
+        for b, (q0, j0) in enumerate([(256, 0), (256, 2), (384, 0), (384, 2)]):
+            late[q0, j0] = psum.tile([P, 2, 128], F32, name=f"acc{q0}_{j0}", tag=f"bank{4 + b}")
+            multiply(late[q0, j0], [j0, j0 + 1], q0, 128, 0)
+
+        for j0 in (0, 2):
+            result = keep.tile([P, 2, 256], F32, name=f"result0_{j0}")
+            for i in range(2):
+                finish(acc_a[j0 + i], [j0 + i], 0, 256, result[:, i : i + 1, :])
+            store(result, j0, 2, 0, 256)
+
+        for q0 in (256, 384):
+            for j0 in (0, 2):
+                multiply(late[q0, j0], [j0, j0 + 1], q0, 128, 1)
+            for j0 in (0, 2):
+                result = keep.tile([P, 2, 128], F32, name=f"result{q0}_{j0}")
+                finish(late[q0, j0], [j0, j0 + 1], q0, 128, result)
+                store(result, j0, 2, q0, 128)

@@ -54,8 +54,8 @@ def tile_attend_neut_silu_kernel(tc, qT, k_words, k_scales, nb, ns, offs, out):
 
         def cast_q(g, q0, width, on_vector=False, first=False):
             grouped[g, q0] = keep.tile([P, width, PACK], BF16, name=f"grouped{g}_{q0}", align_bytes=64)
-            dst = grouped[g, q0][:].rearrange("p (c i) t -> p c t i", i=4)
-            src = raw[g, q0][:].rearrange("p t (c i) -> p c t i", i=4)
+            dst = grouped[g, q0][:]
+            src = raw[g, q0][:].rearrange("p t w -> p w t")
             if on_vector:
                 nc.vector.tensor_copy(dst, src)
             elif first:

@@ -37,7 +37,7 @@ def tile_attend_neut_silu_kernel(tc, qT, k_words, k_scales, nb, ns, offs, out):
 
         offsets = keep.tile([P, N // 16], U16, name="offsets")
         word_pool = keep.tile([P, T], I32, name="word_pool", align_bytes=64)
-        scale_pool = keep.tile([P, T], U8, name="scale_pool")
+        scale_pool = keep.tile([P, T], U8, name="scale_pool", align_bytes=64)
         nb_pool = keep.tile([P, T], F32, name="nb_pool")
         ns_pool = keep.tile([P, T], F32, name="ns_pool")
         ident = keep.tile([P, P], F32, name="ident")
@@ -75,60 +75,53 @@ def tile_attend_neut_silu_kernel(tc, qT, k_words, k_scales, nb, ns, offs, out):
                 q_codes[g, q0 + n0] = codes[:, n0 : n0 + N_MM]
                 q_scales[g, q0 + n0] = scales[:, n0 : n0 + N_MM]
 
-        ns_head = keep.tile([P, 8], F32, name="ns_head")
-        nc.scalar.dma_start(out=ns_head[:], in_=ns[:, 0:8])
-        nc.scalar.dma_start(out=nb_pool[ROW : ROW + 1, :], in_=nb[0:1, :])
-        nc.scalar.dma_start(out=ns_pool[ROW : ROW + 1, :], in_=ns[0:1, :])
         warm = keep.tile([P, 1], F32, name="warm")
         warm_out = keep.tile([P, 1], F32, name="warm_out")
         nc.vector.memset(warm[:], 0.0)
         nc.scalar.activation(warm_out[:], warm[:], SILU)
         nc.vector.memset(scale_pool[:].bitcast(I32), 0)
         nc.vector.memset(nb_pool[0:ROW, :], 0.0)
+        nc.vector.memset(ns_pool[0:ROW, :], 0.0)
         nc.vector.memset(k_scale1[:].bitcast(I32), 0)
         make_identity(nc, ident[:])
 
         nc.sync.dma_start(offsets[:], offs)
+        nc.sync.dma_start(out=nb_pool[ROW : ROW + 1, :], in_=nb[0:1, :])
         load_q(0, 0, 256)
         scale_rows = k_scales.rearrange("o (a r) t -> r a o t", r=4)
         for r in range(4):
             nc.sync.dma_start(out=scale_pool[r:P:SHIFT, :].bitcast(I32), in_=scale_rows[r].bitcast(I32))
+        nc.sync.dma_start(out=ns_pool[ROW : ROW + 1, :], in_=ns[0:1, :])
         nc.sync.dma_start(out=word_pool[:], in_=k_words[0].rearrange("p t b -> p (t b)").bitcast(I32))
         load_q(1, 0, 256)
         load_q(0, 256, 256)
         load_q(1, 256, 128)
         load_q(1, 384, 128)
 
-        nc.scalar.copy(
-            ns_pool[0:ROW, :].rearrange("p (a b) -> p a b", b=8),
-            ns_head[0:ROW, :].unsqueeze(1).to_broadcast([ROW, T // 8, 8]),
-        )
         cast_q(0, 0, 256, first=False)
         nc.vector.tensor_copy(k_scale0[:], scale_pool[:].indirect(offsets[:]))
         nc.scalar.dma_start(out=k_scale1[0 : P - SHIFT, :].bitcast(I32), in_=k_scale0[SHIFT:P, :].bitcast(I32))
 
-        def gather_row(pool, name):
-            listed = keep.tile([P, N], F32, name=name + "_listed")
+        def gather_row(pool, name, tag=None):
+            listed = keep.tile([P, N], F32, name=name + "_listed", align_bytes=64, tag=tag or name + "_listed")
             nc.vector.tensor_copy(listed[:], pool[:].indirect(offsets[:]))
             return listed
 
-        def per_partition(listed, name, bank, tag):
+        def turn(listed, name, bank):
             turned = psum.tile([P, SLOT_TILES, P], F32, name=name + "_turned", tag=bank)
             for j in range(SLOT_TILES):
                 nc.tensor.transpose(turned[:, j, :], listed[:, j * P : (j + 1) * P], ident[:])
-            cols = keep.tile([P, SLOT_TILES], F32, name=name + "_cols", tag=tag)
-            nc.scalar.copy(cols[:], turned[:, :, ROW])
-            return cols
+            return turned
 
-        nb_cols = per_partition(gather_row(nb_pool, "nb"), "nb", "bank4", "nb_cols")
-        ns_listed = gather_row(ns_pool, "ns")
-        pairs = keep.tile([P, N], U32, name="pairs", tag="ns_pool")
+        nb_turned = turn(gather_row(nb_pool, "nb"), "nb", "bank4")
+        quantize_q(0, 0, 256, tag="scale_pool")
+        ns_turned = turn(gather_row(ns_pool, "ns"), "ns", "bank7")
+        pairs = keep.tile([P, N], U32, name="pairs")
         nc.vector.tensor_copy(pairs[:], word_pool[:].bitcast(U32).indirect(offsets[:]))
         k_codes = keep.tile([P, PASSES, 2 * N], U8, name="k_codes", align_bytes=64)
-        nc.vector.tensor_copy(
-            k_codes[:].bitcast(U16), pairs[:].bitcast(U16).rearrange("p (s h) -> p h s", h=PASSES)
-        )
-        quantize_q(0, 0, 256, tag="word_pool")
+        halves = pairs[:].bitcast(U16).rearrange("p (s h) -> p h s", h=PASSES)
+        for g in range(PASSES):
+            nc.vector.tensor_copy(k_codes[:, g, :].bitcast(U16), halves[:, g, :])
 
         def multiply(acc, tiles, q0, width, g):
             sums = [(i, j, n0) for i, j in enumerate(tiles) for n0 in range(0, width, N_MM)]
@@ -147,7 +140,7 @@ def tile_attend_neut_silu_kernel(tc, qT, k_words, k_scales, nb, ns, offs, out):
             for i, j in enumerate(tiles):
                 act = keep.tile([P, width], F32, name=f"act{q0}_{j}")
                 nc.scalar.activation(act[:], acc[:, i, :], SILU, bias=nb_cols[:, j : j + 1])
-                nc.vector.tensor_scalar_mul(result[:, i, :], act[:], ns_cols[:, j : j + 1])
+                nc.vector.tensor_scalar_mul(result[:, i, :], act[:], ns_turned[:, j, ROW:P])
 
         def store(result, j0, count, q0, width):
             rows = out[0, j0 * P : (j0 + count) * P, q0 : q0 + width]
@@ -158,33 +151,42 @@ def tile_attend_neut_silu_kernel(tc, qT, k_words, k_scales, nb, ns, offs, out):
             multiply(acc_a[j], [j], 0, 256, 0)
 
         cast_q(1, 0, 256)
+        nb_cols = keep.tile([P, SLOT_TILES], F32, name="nb_cols", tag="raw1_0")
+        nc.scalar.copy(nb_cols[:], nb_turned[:, :, ROW])
         cast_q(0, 256, 256)
-        ns_cols = per_partition(ns_listed, "ns", "bank5", "raw0_256")
         quantize_q(1, 0, 256)
         for j in range(SLOT_TILES):
             multiply(acc_a[j], [j], 0, 256, 1)
 
         cast_q(1, 256, 128, on_vector=True)
-        quantize_q(1, 256, 128)
         quantize_q(0, 256, 256)
+        quantize_q(1, 256, 128)
         cast_q(1, 384, 128, on_vector=True)
         quantize_q(1, 384, 128)
 
+        act_a = keep.tile([P, SLOT_TILES, 256], F32, name="act_a", tag="raw0_256")
+        for j in range(SLOT_TILES):
+            nc.scalar.activation(act_a[:, j, :], acc_a[j][:, 0, :], SILU, bias=nb_cols[:, j : j + 1])
+
         late = {}
-        for b, (q0, j0) in enumerate([(256, 0), (256, 2), (384, 0), (384, 2)]):
-            late[q0, j0] = psum.tile([P, 2, 128], F32, name=f"acc{q0}_{j0}", tag=f"bank{4 + b}")
-            multiply(late[q0, j0], [j0, j0 + 1], q0, 128, 0)
+        units = [(256, [0, 1, 2, 3]), (384, [0, 1]), (384, [2, 3])]
+        for b, (q0, tiles) in enumerate(units):
+            late[b] = psum.tile([P, len(tiles), 128], F32, name=f"late{b}", tag=f"bank{4 + b}")
+            multiply(late[b], tiles, q0, 128, 0)
+            if b == 0:
+                multiply(late[b], tiles, q0, 128, 1)
 
         for j0 in (0, 2):
             result = keep.tile([P, 2, 256], F32, name=f"result0_{j0}")
             for i in range(2):
-                finish(acc_a[j0 + i], [j0 + i], 0, 256, result[:, i : i + 1, :])
+                j = j0 + i
+                nc.vector.tensor_scalar_mul(result[:, i, :], act_a[:, j, :], ns_turned[:, j, ROW:P])
             store(result, j0, 2, 0, 256)
 
-        for q0 in (256, 384):
-            for j0 in (0, 2):
-                multiply(late[q0, j0], [j0, j0 + 1], q0, 128, 1)
-            for j0 in (0, 2):
-                result = keep.tile([P, 2, 128], F32, name=f"result{q0}_{j0}")
-                finish(late[q0, j0], [j0, j0 + 1], q0, 128, result)
-                store(result, j0, 2, q0, 128)
+        for b, (q0, tiles) in enumerate(units):
+            if b > 0:
+                multiply(late[b], tiles, q0, 128, 1)
+        for b, (q0, tiles) in enumerate(units):
+            result = keep.tile([P, len(tiles), 128], F32, name=f"late_result{b}")
+            finish(late[b], tiles, q0, 128, result)
+            store(result, tiles[0], len(tiles), q0, 128)

@@ -15,7 +15,6 @@ U8 = mybir.dt.uint8
 FP8X4 = mybir.dt.float8_e4m3fn_x4
 FP4X4 = mybir.dt.float4_e2m1fn_x4
 SILU = mybir.ActivationFunctionType.Silu
-COPY = mybir.ActivationFunctionType.Copy
 
 P = 128
 PACK = 4
@@ -25,7 +24,6 @@ SLOT_TILES = N // P
 N_MM = 128
 ROW = P - 1
 SHIFT = 16
-BANK = 512
 
 
 def tile_attend_neut_silu_kernel(tc, qT, k_words, k_scales, nb, ns, offs, out):
@@ -36,10 +34,10 @@ def tile_attend_neut_silu_kernel(tc, qT, k_words, k_scales, nb, ns, offs, out):
         psum = ctx.enter_context(tc.psum_pool(name="psum", bufs=1))
 
         offsets = keep.tile([P, N // 16], U16, name="offsets")
-        word_pool = keep.tile([P, T], I32, name="word_pool", align_bytes=64)
+        word_pool = keep.tile([P, T], I32, name="word_pool", align_bytes=256)
         scale_pool = keep.tile([P, T], U8, name="scale_pool", align_bytes=64)
         nb_pool = keep.tile([P, T], F32, name="nb_pool")
-        ns_pool = keep.tile([P, T], F32, name="ns_pool")
+        ns_pool = keep.tile([P, T], F32, name="ns_pool", align_bytes=64)
         ident = keep.tile([P, P], F32, name="ident")
         k_scale0 = keep.tile([P, N], U8, name="k_scale0", align_bytes=64)
         k_scale1 = keep.tile([P, N], U8, name="k_scale1", align_bytes=64)
@@ -48,20 +46,19 @@ def tile_attend_neut_silu_kernel(tc, qT, k_words, k_scales, nb, ns, offs, out):
         raw, grouped, q_codes, q_scales = {}, {}, {}, {}
 
         def load_q(g, q0, width):
-            raw[g, q0] = keep.tile([P, PACK, width], F32, name=f"raw{g}_{q0}")
+            raw[g, q0] = keep.tile([P, PACK, width], F32, name=f"raw{g}_{q0}", align_bytes=256)
             rows = qT[0, g * K_PASS : (g + 1) * K_PASS, q0 : q0 + width]
             nc.sync.dma_start(out=raw[g, q0][:], in_=rows.rearrange("(p j) w -> p j w", j=PACK))
 
-        def cast_q(g, q0, width, on_vector=False, first=False):
-            grouped[g, q0] = keep.tile([P, width, PACK], BF16, name=f"grouped{g}_{q0}", align_bytes=64)
-            dst = grouped[g, q0][:]
-            src = raw[g, q0][:].rearrange("p t w -> p w t")
-            if on_vector:
-                nc.vector.tensor_copy(dst, src)
-            elif first:
-                nc.scalar.activation(dst, src, COPY)
-            else:
-                nc.scalar.copy(dst, src)
+        on_scalar, on_vector = nc.scalar.copy, nc.vector.tensor_copy
+
+        def cast_q(copy, g, q0, width, part=None):
+            if (g, q0) not in grouped:
+                grouped[g, q0] = keep.tile([P, width, PACK], BF16, name=f"grouped{g}_{q0}", align_bytes=64)
+            a, b = part or (0, width)
+            dst = grouped[g, q0][:, a:b, :].rearrange("p (c i) t -> p c t i", i=4)
+            src = raw[g, q0][:, :, a:b].rearrange("p t (c i) -> p c t i", i=4)
+            copy(dst, src)
 
         def quantize_q(g, q0, width, tag=None):
             codes = keep.tile([P, width], U32, name=f"q_codes{g}_{q0}", align_bytes=64, tag=tag or f"q_codes{g}_{q0}")
@@ -75,17 +72,14 @@ def tile_attend_neut_silu_kernel(tc, qT, k_words, k_scales, nb, ns, offs, out):
                 q_codes[g, q0 + n0] = codes[:, n0 : n0 + N_MM]
                 q_scales[g, q0 + n0] = scales[:, n0 : n0 + N_MM]
 
-        warm = keep.tile([P, 1], F32, name="warm")
-        warm_out = keep.tile([P, 1], F32, name="warm_out")
-        nc.vector.memset(warm[:], 0.0)
-        nc.scalar.activation(warm_out[:], warm[:], SILU)
+        ns_head = keep.tile([P, 8], F32, name="ns_head")
         nc.vector.memset(scale_pool[:].bitcast(I32), 0)
         nc.vector.memset(nb_pool[0:ROW, :], 0.0)
-        nc.vector.memset(ns_pool[0:ROW, :], 0.0)
         nc.vector.memset(k_scale1[:].bitcast(I32), 0)
         make_identity(nc, ident[:])
 
         nc.sync.dma_start(offsets[:], offs)
+        nc.sync.dma_start(out=ns_head[:], in_=ns[:, 0:8])
         nc.sync.dma_start(out=nb_pool[ROW : ROW + 1, :], in_=nb[0:1, :])
         load_q(0, 0, 256)
         scale_rows = k_scales.rearrange("o (a r) t -> r a o t", r=4)
@@ -98,7 +92,13 @@ def tile_attend_neut_silu_kernel(tc, qT, k_words, k_scales, nb, ns, offs, out):
         load_q(1, 256, 128)
         load_q(1, 384, 128)
 
-        cast_q(0, 0, 256, first=False)
+        warm_out = keep.tile([P, 1], F32, name="warm_out")
+        nc.scalar.activation(warm_out[:], ns_head[:, 0:1], SILU)
+        nc.scalar.copy(
+            ns_pool[0:ROW, :].rearrange("p (a b) -> p a b", b=8),
+            ns_head[0:ROW, :].unsqueeze(1).to_broadcast([ROW, T // 8, 8]),
+        )
+        cast_q(on_scalar, 0, 0, 256)
         nc.vector.tensor_copy(k_scale0[:], scale_pool[:].indirect(offsets[:]))
         nc.scalar.dma_start(out=k_scale1[0 : P - SHIFT, :].bitcast(I32), in_=k_scale0[SHIFT:P, :].bitcast(I32))
 
@@ -114,8 +114,8 @@ def tile_attend_neut_silu_kernel(tc, qT, k_words, k_scales, nb, ns, offs, out):
             return turned
 
         nb_turned = turn(gather_row(nb_pool, "nb"), "nb", "bank4")
-        quantize_q(0, 0, 256, tag="scale_pool")
         ns_turned = turn(gather_row(ns_pool, "ns"), "ns", "bank7")
+        quantize_q(0, 0, 256, tag="ns_pool")
         pairs = keep.tile([P, N], U32, name="pairs")
         nc.vector.tensor_copy(pairs[:], word_pool[:].bitcast(U32).indirect(offsets[:]))
         k_codes = keep.tile([P, PASSES, 2 * N], U8, name="k_codes", align_bytes=64)
@@ -150,21 +150,22 @@ def tile_attend_neut_silu_kernel(tc, qT, k_words, k_scales, nb, ns, offs, out):
         for j in range(SLOT_TILES):
             multiply(acc_a[j], [j], 0, 256, 0)
 
-        cast_q(1, 0, 256)
-        nb_cols = keep.tile([P, SLOT_TILES], F32, name="nb_cols", tag="raw1_0")
+        cast_q(on_scalar, 1, 0, 256)
+        nb_cols = keep.tile([P, SLOT_TILES], F32, name="nb_cols", tag="raw1_0", align_bytes=256)
         nc.scalar.copy(nb_cols[:], nb_turned[:, :, ROW])
-        cast_q(0, 256, 256)
+        cast_q(on_scalar, 0, 256, 256, part=(0, 128))
         quantize_q(1, 0, 256)
         for j in range(SLOT_TILES):
             multiply(acc_a[j], [j], 0, 256, 1)
 
-        cast_q(1, 256, 128, on_vector=True)
+        cast_q(on_vector, 0, 256, 256, part=(128, 256))
         quantize_q(0, 256, 256)
+        cast_q(on_vector, 1, 256, 128)
         quantize_q(1, 256, 128)
-        cast_q(1, 384, 128, on_vector=True)
+        cast_q(on_vector, 1, 384, 128)
         quantize_q(1, 384, 128)
 
-        act_a = keep.tile([P, SLOT_TILES, 256], F32, name="act_a", tag="raw0_256")
+        act_a = keep.tile([P, SLOT_TILES, 256], F32, name="act_a", tag="raw0_256", align_bytes=256)
         for j in range(SLOT_TILES):
             nc.scalar.activation(act_a[:, j, :], acc_a[j][:, 0, :], SILU, bias=nb_cols[:, j : j + 1])
 
@@ -177,7 +178,7 @@ def tile_attend_neut_silu_kernel(tc, qT, k_words, k_scales, nb, ns, offs, out):
                 multiply(late[b], tiles, q0, 128, 1)
 
         for j0 in (0, 2):
-            result = keep.tile([P, 2, 256], F32, name=f"result0_{j0}")
+            result = keep.tile([P, 2, 256], F32, name=f"result0_{j0}", align_bytes=256)
             for i in range(2):
                 j = j0 + i
                 nc.vector.tensor_scalar_mul(result[:, i, :], act_a[:, j, :], ns_turned[:, j, ROW:P])
@@ -187,6 +188,6 @@ def tile_attend_neut_silu_kernel(tc, qT, k_words, k_scales, nb, ns, offs, out):
             if b > 0:
                 multiply(late[b], tiles, q0, 128, 1)
         for b, (q0, tiles) in enumerate(units):
-            result = keep.tile([P, len(tiles), 128], F32, name=f"late_result{b}")
+            result = keep.tile([P, len(tiles), 128], F32, name=f"late_result{b}", align_bytes=256)
             finish(late[b], tiles, q0, 128, result)
             store(result, tiles[0], len(tiles), q0, 128)

@@ -88,9 +88,6 @@ def tile_attend_neut_silu_kernel(tc, qT, k_words, k_scales, nb, ns, offs, out):
         nc.sync.dma_start(out=ns_pool[ROW : ROW + 1, :], in_=ns[0:1, :])
         nc.sync.dma_start(out=word_pool[:], in_=k_words[0].rearrange("p t b -> p (t b)").bitcast(I32))
         load_q(1, 0, 256)
-        load_q(0, 256, 256)
-        load_q(1, 256, 128)
-        load_q(1, 384, 128)
 
         warm_out = keep.tile([P, 1], F32, name="warm_out")
         nc.scalar.activation(warm_out[:], ns_head[:, 0:1], SILU)
@@ -100,7 +97,10 @@ def tile_attend_neut_silu_kernel(tc, qT, k_words, k_scales, nb, ns, offs, out):
         )
         cast_q(on_scalar, 0, 0, 256)
         nc.vector.tensor_copy(k_scale0[:], scale_pool[:].indirect(offsets[:]))
-        nc.scalar.dma_start(out=k_scale1[0 : P - SHIFT, :].bitcast(I32), in_=k_scale0[SHIFT:P, :].bitcast(I32))
+        nc.sync.dma_start(out=k_scale1[0 : P - SHIFT, :].bitcast(I32), in_=k_scale0[SHIFT:P, :].bitcast(I32))
+        load_q(0, 256, 256)
+        load_q(1, 256, 128)
+        load_q(1, 384, 128)
 
         def gather_row(pool, name, tag=None):
             listed = keep.tile([P, N], F32, name=name + "_listed", align_bytes=64, tag=tag or name + "_listed")
@@ -114,7 +114,11 @@ def tile_attend_neut_silu_kernel(tc, qT, k_words, k_scales, nb, ns, offs, out):
             return turned
 
         nb_turned = turn(gather_row(nb_pool, "nb"), "nb", "bank4")
-        ns_turned = turn(gather_row(ns_pool, "ns"), "ns", "bank7")
+        nb_cols = keep.tile([P, SLOT_TILES], F32, name="nb_cols", tag="raw0_0", align_bytes=256)
+        nc.scalar.copy(nb_cols[:], nb_turned[:, :, ROW])
+        ns_turned = turn(gather_row(ns_pool, "ns"), "ns", "bank5")
+        ns_cols = keep.tile([P, SLOT_TILES], F32, name="ns_cols")
+        nc.scalar.copy(ns_cols[:], ns_turned[:, :, ROW])
         quantize_q(0, 0, 256, tag="ns_pool")
         pairs = keep.tile([P, N], U32, name="pairs")
         nc.vector.tensor_copy(pairs[:], word_pool[:].bitcast(U32).indirect(offsets[:]))
@@ -140,7 +144,7 @@ def tile_attend_neut_silu_kernel(tc, qT, k_words, k_scales, nb, ns, offs, out):
             for i, j in enumerate(tiles):
                 act = keep.tile([P, width], F32, name=f"act{q0}_{j}")
                 nc.scalar.activation(act[:], acc[:, i, :], SILU, bias=nb_cols[:, j : j + 1])
-                nc.vector.tensor_scalar_mul(result[:, i, :], act[:], ns_turned[:, j, ROW:P])
+                nc.vector.tensor_scalar_mul(result[:, i, :], act[:], ns_cols[:, j : j + 1])
 
         def store(result, j0, count, q0, width):
             rows = out[0, j0 * P : (j0 + count) * P, q0 : q0 + width]
@@ -151,8 +155,6 @@ def tile_attend_neut_silu_kernel(tc, qT, k_words, k_scales, nb, ns, offs, out):
             multiply(acc_a[j], [j], 0, 256, 0)
 
         cast_q(on_scalar, 1, 0, 256)
-        nb_cols = keep.tile([P, SLOT_TILES], F32, name="nb_cols", tag="raw1_0", align_bytes=256)
-        nc.scalar.copy(nb_cols[:], nb_turned[:, :, ROW])
         cast_q(on_scalar, 0, 256, 256, part=(0, 128))
         quantize_q(1, 0, 256)
         for j in range(SLOT_TILES):
@@ -170,7 +172,7 @@ def tile_attend_neut_silu_kernel(tc, qT, k_words, k_scales, nb, ns, offs, out):
             nc.scalar.activation(act_a[:, j, :], acc_a[j][:, 0, :], SILU, bias=nb_cols[:, j : j + 1])
 
         late = {}
-        units = [(256, [0, 1, 2, 3]), (384, [0, 1]), (384, [2, 3])]
+        units = [(256, [0, 1, 2, 3]), (384, [0, 1]), (384, [2]), (384, [3])]
         for b, (q0, tiles) in enumerate(units):
             late[b] = psum.tile([P, len(tiles), 128], F32, name=f"late{b}", tag=f"bank{4 + b}")
             multiply(late[b], tiles, q0, 128, 0)
@@ -181,7 +183,7 @@ def tile_attend_neut_silu_kernel(tc, qT, k_words, k_scales, nb, ns, offs, out):
             result = keep.tile([P, 2, 256], F32, name=f"result0_{j0}", align_bytes=256)
             for i in range(2):
                 j = j0 + i
-                nc.vector.tensor_scalar_mul(result[:, i, :], act_a[:, j, :], ns_turned[:, j, ROW:P])
+                nc.vector.tensor_scalar_mul(result[:, i, :], act_a[:, j, :], ns_cols[:, j : j + 1])
             store(result, j0, 2, 0, 256)
 
         for b, (q0, tiles) in enumerate(units):

@@ -43,7 +43,7 @@ def tile_attend_neut_silu_kernel(tc, qT, k_words, k_scales, nb, ns, offs, out):
         k_scale1 = keep.tile([P, N], U8, name="k_scale1", align_bytes=64)
         k_scale = [k_scale0, k_scale1]
 
-        raw, grouped, q_codes, q_scales = {}, {}, {}, {}
+        raw, q_codes, q_scales = {}, {}, {}
 
         def load_q(g, q0, width):
             raw[g, q0] = keep.tile([P, PACK, width], F32, name=f"raw{g}_{q0}", align_bytes=256)
@@ -52,25 +52,25 @@ def tile_attend_neut_silu_kernel(tc, qT, k_words, k_scales, nb, ns, offs, out):
 
         on_scalar, on_vector = nc.scalar.copy, nc.vector.tensor_copy
 
-        def cast_q(copy, g, q0, width, part=None):
-            if (g, q0) not in grouped:
-                grouped[g, q0] = keep.tile([P, width, PACK], BF16, name=f"grouped{g}_{q0}", align_bytes=64)
-            a, b = part or (0, width)
-            dst = grouped[g, q0][:, a:b, :].rearrange("p (c i) t -> p c t i", i=4)
-            src = raw[g, q0][:, :, a:b].rearrange("p t (c i) -> p c t i", i=4)
-            copy(dst, src)
+        def stage(name):
+            return keep.tile([P, 2 * N_MM, PACK], BF16, name=name, align_bytes=256)
 
-        def quantize_q(g, q0, width, tag=None):
-            codes = keep.tile([P, width], U32, name=f"q_codes{g}_{q0}", align_bytes=64, tag=tag or f"q_codes{g}_{q0}")
-            scales = keep.tile([P, width], U8, name=f"q_scales{g}_{q0}", align_bytes=64)
+        def cast_q(copy, staged, at, g, q0, width, loaded):
+            dst = staged[:, at : at + width, :]
+            src = raw[g, loaded][:, :, q0 - loaded : q0 - loaded + width]
+            copy(dst.rearrange("p (c i) t -> p c t i", i=4), src.rearrange("p t (c i) -> p c t i", i=4))
+
+        def quantize_q(staged, name, blocks, tag=None):
+            codes = keep.tile([P, 2 * N_MM], U32, name=name + "_codes", align_bytes=64, tag=tag or name + "_codes")
+            scales = keep.tile([P, 2 * N_MM], U8, name=name + "_scales", align_bytes=64)
             nc.vector.quantize_mx(
                 out=codes[:].bitcast(FP8X4),
                 scales=scales[:],
-                in_=grouped[g, q0][:].rearrange("p w j -> p (w j)"),
+                in_=staged[:].rearrange("p w j -> p (w j)"),
             )
-            for n0 in range(0, width, N_MM):
-                q_codes[g, q0 + n0] = codes[:, n0 : n0 + N_MM]
-                q_scales[g, q0 + n0] = scales[:, n0 : n0 + N_MM]
+            for i, block in enumerate(blocks):
+                q_codes[block] = codes[:, i * N_MM : (i + 1) * N_MM]
+                q_scales[block] = scales[:, i * N_MM : (i + 1) * N_MM]
 
         ns_head = keep.tile([P, 8], F32, name="ns_head")
         nc.vector.memset(scale_pool[:].bitcast(I32), 0)
@@ -95,10 +95,11 @@ def tile_attend_neut_silu_kernel(tc, qT, k_words, k_scales, nb, ns, offs, out):
             ns_pool[0:ROW, :].rearrange("p (a b) -> p a b", b=8),
             ns_head[0:ROW, :].unsqueeze(1).to_broadcast([ROW, T // 8, 8]),
         )
-        cast_q(on_scalar, 0, 0, 256)
+        first0 = stage("first0")
+        cast_q(on_scalar, first0, 0, 0, 0, 256, 0)
         nc.vector.tensor_copy(k_scale0[:], scale_pool[:].indirect(offsets[:]))
-        nc.sync.dma_start(out=k_scale1[0 : P - SHIFT, :].bitcast(I32), in_=k_scale0[SHIFT:P, :].bitcast(I32))
         load_q(0, 256, 256)
+        nc.sync.dma_start(out=k_scale1[0 : P - SHIFT, :].bitcast(I32), in_=k_scale0[SHIFT:P, :].bitcast(I32))
         load_q(1, 256, 128)
         load_q(1, 384, 128)
 
@@ -119,20 +120,24 @@ def tile_attend_neut_silu_kernel(tc, qT, k_words, k_scales, nb, ns, offs, out):
         ns_turned = turn(gather_row(ns_pool, "ns"), "ns", "bank5")
         ns_cols = keep.tile([P, SLOT_TILES], F32, name="ns_cols")
         nc.scalar.copy(ns_cols[:], ns_turned[:, :, ROW])
-        quantize_q(0, 0, 256, tag="ns_pool")
+        quantize_q(first0, "first0", [(0, 0), (0, 128)], tag="ns_pool")
         pairs = keep.tile([P, N], U32, name="pairs")
         nc.vector.tensor_copy(pairs[:], word_pool[:].bitcast(U32).indirect(offsets[:]))
-        k_codes = keep.tile([P, PASSES, 2 * N], U8, name="k_codes", align_bytes=64)
         halves = pairs[:].bitcast(U16).rearrange("p (s h) -> p h s", h=PASSES)
-        for g in range(PASSES):
-            nc.vector.tensor_copy(k_codes[:, g, :].bitcast(U16), halves[:, g, :])
+        k_codes = {}
+
+        def part_words(g, tag):
+            k_codes[g] = keep.tile([P, 2 * N], U8, name=f"k_codes{g}", tag=tag, align_bytes=256)
+            nc.vector.tensor_copy(k_codes[g][:].bitcast(U16), halves[:, g, :])
+
+        part_words(0, "k_codes0")
 
         def multiply(acc, tiles, q0, width, g):
             sums = [(i, j, n0) for i, j in enumerate(tiles) for n0 in range(0, width, N_MM)]
             for s, (i, j, n0) in enumerate(sums):
                 nc.tensor.matmul_mx(
                     out=acc[:, i, n0 : n0 + N_MM],
-                    lhsT=k_codes[:, g, 2 * P * j : 2 * P * (j + 1)].bitcast(FP4X4),
+                    lhsT=k_codes[g][:, 2 * P * j : 2 * P * (j + 1)].bitcast(FP4X4),
                     lhsT_scale=k_scale[g][:, P * j : P * (j + 1)],
                     rhs=q_codes[g, q0 + n0].bitcast(FP8X4),
                     rhs_scale=q_scales[g, q0 + n0],
@@ -148,48 +153,49 @@ def tile_attend_neut_silu_kernel(tc, qT, k_words, k_scales, nb, ns, offs, out):
 
         def store(result, j0, count, q0, width):
             rows = out[0, j0 * P : (j0 + count) * P, q0 : q0 + width]
-            nc.sync.dma_start(out=rows.rearrange("(j p) w -> p j w", p=P), in_=result[:])
+            nc.sync.dma_start(out=rows.rearrange("(j p) w -> p j w", p=P), in_=result)
 
         acc_a = [psum.tile([P, 1, 256], F32, name=f"acc_a{j}", tag=f"bank{j}") for j in range(SLOT_TILES)]
         for j in range(SLOT_TILES):
             multiply(acc_a[j], [j], 0, 256, 0)
 
-        cast_q(on_scalar, 1, 0, 256)
-        cast_q(on_scalar, 0, 256, 256, part=(0, 128))
-        quantize_q(1, 0, 256)
+        first1 = stage("first1")
+        cast_q(on_scalar, first1, 128, 1, 128, 128, 0)
+        cast_q(on_vector, first1, 0, 1, 0, 128, 0)
+        part_words(1, "raw1_0")
+        quantize_q(first1, "first1", [(1, 0), (1, 128)])
+        second, third = stage("second"), stage("third")
+        cast_q(on_scalar, second, 0, 0, 256, 128, 256)
+        cast_q(on_scalar, third, 0, 0, 384, 128, 256)
         for j in range(SLOT_TILES):
             multiply(acc_a[j], [j], 0, 256, 1)
 
-        cast_q(on_vector, 0, 256, 256, part=(128, 256))
-        quantize_q(0, 256, 256)
-        cast_q(on_vector, 1, 256, 128)
-        quantize_q(1, 256, 128)
-        cast_q(on_vector, 1, 384, 128)
-        quantize_q(1, 384, 128)
+        cast_q(on_vector, second, 128, 1, 256, 128, 256)
+        quantize_q(second, "second", [(0, 256), (1, 256)])
+        cast_q(on_vector, third, 128, 1, 384, 128, 384)
+        quantize_q(third, "third", [(0, 384), (1, 384)])
 
-        act_a = keep.tile([P, SLOT_TILES, 256], F32, name="act_a", tag="raw0_256", align_bytes=256)
+        act_a = keep.tile([P, SLOT_TILES, 256], F32, name="act_a", align_bytes=256)
         for j in range(SLOT_TILES):
             nc.scalar.activation(act_a[:, j, :], acc_a[j][:, 0, :], SILU, bias=nb_cols[:, j : j + 1])
 
         late = {}
-        units = [(256, [0, 1, 2, 3]), (384, [0, 1]), (384, [2]), (384, [3])]
+        units = [(256, [0, 1]), (256, [2, 3]), (384, [0, 1]), (384, [2, 3])]
         for b, (q0, tiles) in enumerate(units):
             late[b] = psum.tile([P, len(tiles), 128], F32, name=f"late{b}", tag=f"bank{4 + b}")
-            multiply(late[b], tiles, q0, 128, 0)
-            if b == 0:
-                multiply(late[b], tiles, q0, 128, 1)
+            for g in range(PASSES):
+                multiply(late[b], tiles, q0, 128, g)
 
-        for j0 in (0, 2):
-            result = keep.tile([P, 2, 256], F32, name=f"result0_{j0}", align_bytes=256)
-            for i in range(2):
-                j = j0 + i
+        early = keep.tile([P, 1, 256], F32, name="early_result", tag="raw1_384", align_bytes=256)
+        rest = keep.tile([P, SLOT_TILES - 1, 256], F32, name="rest_result", tag="third", align_bytes=256)
+        for result, group in ((early[:], [0]), (rest[:, 0:1, :], [1]), (rest[:, 1:3, :], [2, 3])):
+            for i, j in enumerate(group):
                 nc.vector.tensor_scalar_mul(result[:, i, :], act_a[:, j, :], ns_cols[:, j : j + 1])
-            store(result, j0, 2, 0, 256)
+            store(result, group[0], len(group), 0, 256)
 
         for b, (q0, tiles) in enumerate(units):
-            if b > 0:
-                multiply(late[b], tiles, q0, 128, 1)
-        for b, (q0, tiles) in enumerate(units):
-            result = keep.tile([P, len(tiles), 128], F32, name=f"late_result{b}", align_bytes=256)
-            finish(late[b], tiles, q0, 128, result)
-            store(result, tiles[0], len(tiles), q0, 128)
+            groups = [tiles] if b < len(units) - 1 else [[j] for j in tiles]
+            for group in groups:
+                result = keep.tile([P, len(group), 128], F32, name=f"late_result{q0}_{group[0]}", align_bytes=256)
+                finish(late[b][:, group[0] - tiles[0] :, :], group, q0, 128, result)
+                store(result[:], group[0], len(group), q0, 128)

@@ -23,7 +23,8 @@ PASSES = D // K_PASS
 SLOT_TILES = N // P
 N_MM = 128
 ROW = P - 1
-SHIFT = 16
+SCALE_ROWS = 16
+SCALE_STEP = 4
 
 
 def tile_attend_neut_silu_kernel(tc, qT, k_words, k_scales, nb, ns, offs, out):
@@ -35,13 +36,12 @@ def tile_attend_neut_silu_kernel(tc, qT, k_words, k_scales, nb, ns, offs, out):
 
         offsets = keep.tile([P, N // 16], U16, name="offsets")
         word_pool = keep.tile([P, T], I32, name="word_pool", align_bytes=256)
-        scale_pool = keep.tile([P, T], U8, name="scale_pool", align_bytes=64)
+        scale_pool = keep.tile([P, PASSES, T], U8, name="scale_pool", align_bytes=256)
         nb_pool = keep.tile([P, T], F32, name="nb_pool")
         ns_pool = keep.tile([P, T], F32, name="ns_pool", align_bytes=64)
         ident = keep.tile([P, P], F32, name="ident")
-        k_scale0 = keep.tile([P, N], U8, name="k_scale0", align_bytes=64)
-        k_scale1 = keep.tile([P, N], U8, name="k_scale1", align_bytes=64)
-        k_scale = [k_scale0, k_scale1]
+        scale_listed = keep.tile([P, PASSES, N], U8, name="scale_listed", align_bytes=256)
+        k_scale = keep.tile([P, PASSES, N], U8, name="k_scale", align_bytes=256)
 
         raw, q_codes, q_scales = {}, {}, {}
 
@@ -75,17 +75,18 @@ def tile_attend_neut_silu_kernel(tc, qT, k_words, k_scales, nb, ns, offs, out):
         ns_head = keep.tile([P, 8], F32, name="ns_head")
         nc.vector.memset(scale_pool[:].bitcast(I32), 0)
         nc.vector.memset(nb_pool[0:ROW, :], 0.0)
-        nc.vector.memset(k_scale1[:].bitcast(I32), 0)
+        nc.vector.memset(k_scale[:].bitcast(I32), 0)
         make_identity(nc, ident[:])
 
         nc.sync.dma_start(offsets[:], offs)
         nc.sync.dma_start(out=ns_head[:], in_=ns[:, 0:8])
         nc.sync.dma_start(out=nb_pool[ROW : ROW + 1, :], in_=nb[0:1, :])
-        load_q(0, 0, 256)
-        scale_rows = k_scales.rearrange("o (a r) t -> r a o t", r=4)
-        for r in range(4):
-            nc.sync.dma_start(out=scale_pool[r:P:SHIFT, :].bitcast(I32), in_=scale_rows[r].bitcast(I32))
+        nc.sync.dma_start(
+            out=scale_pool[0 : SCALE_ROWS * SCALE_STEP : SCALE_STEP].bitcast(I32),
+            in_=k_scales.rearrange("o f t -> f o t").bitcast(I32),
+        )
         nc.sync.dma_start(out=ns_pool[ROW : ROW + 1, :], in_=ns[0:1, :])
+        load_q(0, 0, 256)
         nc.sync.dma_start(out=word_pool[:], in_=k_words[0].rearrange("p t b -> p (t b)").bitcast(I32))
         load_q(1, 0, 256)
 
@@ -97,9 +98,12 @@ def tile_attend_neut_silu_kernel(tc, qT, k_words, k_scales, nb, ns, offs, out):
         )
         first0 = stage("first0")
         cast_q(on_scalar, first0, 0, 0, 0, 256, 0)
-        nc.vector.tensor_copy(k_scale0[:], scale_pool[:].indirect(offsets[:]))
+        for g in range(PASSES):
+            nc.vector.tensor_copy(scale_listed[:, g, :], scale_pool[:, g, :].indirect(offsets[:]))
+        for r in range(4):
+            rows = scale_listed[SCALE_STEP * r : SCALE_ROWS * SCALE_STEP : 4 * SCALE_STEP]
+            nc.sync.dma_start(out=k_scale[r:P:32].bitcast(I32), in_=rows.bitcast(I32))
         load_q(0, 256, 256)
-        nc.sync.dma_start(out=k_scale1[0 : P - SHIFT, :].bitcast(I32), in_=k_scale0[SHIFT:P, :].bitcast(I32))
         load_q(1, 256, 128)
         load_q(1, 384, 128)
 
@@ -115,11 +119,11 @@ def tile_attend_neut_silu_kernel(tc, qT, k_words, k_scales, nb, ns, offs, out):
             return turned
 
         nb_turned = turn(gather_row(nb_pool, "nb"), "nb", "bank4")
-        nb_cols = keep.tile([P, SLOT_TILES], F32, name="nb_cols", tag="raw0_0", align_bytes=256)
-        nc.scalar.copy(nb_cols[:], nb_turned[:, :, ROW])
+        columns = keep.tile([P, 2, SLOT_TILES], F32, name="columns", tag="raw0_0", align_bytes=256)
+        nb_cols, ns_cols = columns[:, 0, :], columns[:, 1, :]
+        nc.scalar.copy(nb_cols, nb_turned[:, :, ROW])
         ns_turned = turn(gather_row(ns_pool, "ns"), "ns", "bank5")
-        ns_cols = keep.tile([P, SLOT_TILES], F32, name="ns_cols")
-        nc.scalar.copy(ns_cols[:], ns_turned[:, :, ROW])
+        nc.scalar.copy(ns_cols, ns_turned[:, :, ROW])
         quantize_q(first0, "first0", [(0, 0), (0, 128)], tag="ns_pool")
         pairs = keep.tile([P, N], U32, name="pairs")
         nc.vector.tensor_copy(pairs[:], word_pool[:].bitcast(U32).indirect(offsets[:]))
@@ -138,7 +142,7 @@ def tile_attend_neut_silu_kernel(tc, qT, k_words, k_scales, nb, ns, offs, out):
                 nc.tensor.matmul_mx(
                     out=acc[:, i, n0 : n0 + N_MM],
                     lhsT=k_codes[g][:, 2 * P * j : 2 * P * (j + 1)].bitcast(FP4X4),
-                    lhsT_scale=k_scale[g][:, P * j : P * (j + 1)],
+                    lhsT_scale=k_scale[:, g, P * j : P * (j + 1)],
                     rhs=q_codes[g, q0 + n0].bitcast(FP8X4),
                     rhs_scale=q_scales[g, q0 + n0],
                     start=(g == 0 and s == 0),
@@ -175,7 +179,7 @@ def tile_attend_neut_silu_kernel(tc, qT, k_words, k_scales, nb, ns, offs, out):
         cast_q(on_vector, third, 128, 1, 384, 128, 384)
         quantize_q(third, "third", [(0, 384), (1, 384)])
 
-        act_a = keep.tile([P, SLOT_TILES, 256], F32, name="act_a", align_bytes=256)
+        act_a = keep.tile([P, SLOT_TILES, 256], F32, name="act_a", tag="raw0_256", align_bytes=256)
         for j in range(SLOT_TILES):
             nc.scalar.activation(act_a[:, j, :], acc_a[j][:, 0, :], SILU, bias=nb_cols[:, j : j + 1])
 

@@ -89,6 +89,7 @@ def tile_attend_neut_silu_kernel(tc, qT, k_words, k_scales, nb, ns, offs, out):
         load_q(0, 0, 256)
         nc.sync.dma_start(out=word_pool[:], in_=k_words[0].rearrange("p t b -> p (t b)").bitcast(I32))
         load_q(1, 0, 256)
+        load_q(1, 256, 128)
 
         warm_out = keep.tile([P, 1], F32, name="warm_out")
         nc.scalar.activation(warm_out[:], ns_head[:, 0:1], SILU)
@@ -104,7 +105,6 @@ def tile_attend_neut_silu_kernel(tc, qT, k_words, k_scales, nb, ns, offs, out):
             rows = scale_listed[SCALE_STEP * r : SCALE_ROWS * SCALE_STEP : 4 * SCALE_STEP]
             nc.sync.dma_start(out=k_scale[r:P:32].bitcast(I32), in_=rows.bitcast(I32))
         load_q(0, 256, 256)
-        load_q(1, 256, 128)
         load_q(1, 384, 128)
 
         def gather_row(pool, name, tag=None):
@@ -164,17 +164,16 @@ def tile_attend_neut_silu_kernel(tc, qT, k_words, k_scales, nb, ns, offs, out):
             multiply(acc_a[j], [j], 0, 256, 0)
 
         first1 = stage("first1")
-        cast_q(on_scalar, first1, 128, 1, 128, 128, 0)
-        cast_q(on_vector, first1, 0, 1, 0, 128, 0)
-        part_words(1, "raw1_0")
+        cast_q(on_scalar, first1, 0, 1, 0, 256, 0)
+        part_words(1, "k_codes1")
         quantize_q(first1, "first1", [(1, 0), (1, 128)])
         second, third = stage("second"), stage("third")
         cast_q(on_scalar, second, 0, 0, 256, 128, 256)
-        cast_q(on_scalar, third, 0, 0, 384, 128, 256)
         for j in range(SLOT_TILES):
             multiply(acc_a[j], [j], 0, 256, 1)
 
         cast_q(on_vector, second, 128, 1, 256, 128, 256)
+        cast_q(on_vector, third, 0, 0, 384, 128, 256)
         quantize_q(second, "second", [(0, 256), (1, 256)])
         cast_q(on_vector, third, 128, 1, 384, 128, 384)
         quantize_q(third, "third", [(0, 384), (1, 384)])
@@ -192,10 +191,10 @@ def tile_attend_neut_silu_kernel(tc, qT, k_words, k_scales, nb, ns, offs, out):
 
         early = keep.tile([P, 1, 256], F32, name="early_result", tag="raw1_384", align_bytes=256)
         rest = keep.tile([P, SLOT_TILES - 1, 256], F32, name="rest_result", tag="third", align_bytes=256)
-        for result, group in ((early[:], [0]), (rest[:, 0:1, :], [1]), (rest[:, 1:3, :], [2, 3])):
-            for i, j in enumerate(group):
-                nc.vector.tensor_scalar_mul(result[:, i, :], act_a[:, j, :], ns_cols[:, j : j + 1])
-            store(result, group[0], len(group), 0, 256)
+        for j in range(SLOT_TILES):
+            result = rest[:, j - 1 : j, :] if j else early[:]
+            nc.vector.tensor_scalar_mul(result[:, 0, :], act_a[:, j, :], ns_cols[:, j : j + 1])
+            store(result, j, 1, 0, 256)
 
         for b, (q0, tiles) in enumerate(units):
             groups = [tiles] if b < len(units) - 1 else [[j] for j in tiles]

@@ -21,10 +21,9 @@ PACK = 4
 K_PASS = P * PACK
 PASSES = D // K_PASS
 SLOT_TILES = N // P
-N_MM = 128
 ROW = P - 1
-SCALE_ROWS = 16
 SCALE_STEP = 4
+KIB = 1024
 
 
 def tile_attend_neut_silu_kernel(tc, qT, k_words, k_scales, nb, ns, offs, out):
@@ -32,173 +31,153 @@ def tile_attend_neut_silu_kernel(tc, qT, k_words, k_scales, nb, ns, offs, out):
 
     with ExitStack() as ctx:
         keep = ctx.enter_context(tc.tile_pool(name="keep", bufs=1))
+        reuse = ctx.enter_context(tc.tile_pool(name="reuse", bufs=1))
         psum = ctx.enter_context(tc.psum_pool(name="psum", bufs=1))
 
         offsets = keep.tile([P, N // 16], U16, name="offsets")
         word_pool = keep.tile([P, T], I32, name="word_pool", align_bytes=256)
-        scale_pool = keep.tile([P, PASSES, T], U8, name="scale_pool", align_bytes=256)
-        nb_pool = keep.tile([P, T], F32, name="nb_pool")
-        ns_pool = keep.tile([P, T], F32, name="ns_pool", align_bytes=64)
+        scale_pool = reuse.tile([P, T], U8, name="scale_pool", align_bytes=256, offset=0)
+        nb_pool = reuse.tile([P, T], F32, name="nb_pool", align_bytes=256, offset=4 * KIB)
+        ns_pool = reuse.tile([P, T], F32, name="ns_pool", align_bytes=256, offset=12 * KIB)
         ident = keep.tile([P, P], F32, name="ident")
-        scale_listed = keep.tile([P, PASSES, N], U8, name="scale_listed", align_bytes=256)
+        scale_listed = keep.tile([P, N], U8, name="scale_listed", align_bytes=256)
         k_scale = keep.tile([P, PASSES, N], U8, name="k_scale", align_bytes=256)
 
-        raw, q_codes, q_scales = {}, {}, {}
-
-        def load_q(g, q0, width):
-            raw[g, q0] = keep.tile([P, PACK, width], F32, name=f"raw{g}_{q0}", align_bytes=256)
+        def load_q(g, q0, width, offset):
+            raw = reuse.tile([P, PACK, width], F32, name=f"raw{g}_{q0}", align_bytes=256, offset=offset)
             rows = qT[0, g * K_PASS : (g + 1) * K_PASS, q0 : q0 + width]
-            nc.sync.dma_start(out=raw[g, q0][:], in_=rows.rearrange("(p j) w -> p j w", j=PACK))
+            nc.sync.dma_start(out=raw[:], in_=rows.rearrange("(p j) w -> p j w", j=PACK))
+            return raw
 
         on_scalar, on_vector = nc.scalar.copy, nc.vector.tensor_copy
 
-        def stage(name):
-            return keep.tile([P, 2 * N_MM, PACK], BF16, name=name, align_bytes=256)
+        def cast_q(copy, staged, raw, c0, c1):
+            copy(
+                staged[:, c0:c1, :].rearrange("p (c i) t -> p c t i", i=4),
+                raw[:, :, c0:c1].rearrange("p t (c i) -> p c t i", i=4),
+            )
 
-        def cast_q(copy, staged, at, g, q0, width, loaded):
-            dst = staged[:, at : at + width, :]
-            src = raw[g, loaded][:, :, q0 - loaded : q0 - loaded + width]
-            copy(dst.rearrange("p (c i) t -> p c t i", i=4), src.rearrange("p t (c i) -> p c t i", i=4))
+        def stage(name, width):
+            return keep.tile([P, width, PACK], BF16, name=name, align_bytes=256)
 
-        def quantize_q(staged, name, blocks, tag=None):
-            codes = keep.tile([P, 2 * N_MM], U32, name=name + "_codes", align_bytes=64, tag=tag or name + "_codes")
-            scales = keep.tile([P, 2 * N_MM], U8, name=name + "_scales", align_bytes=64)
+        def quantize_q(staged, name, width):
+            codes = keep.tile([P, width], U32, name=name + "_codes", align_bytes=256)
+            scales = keep.tile([P, width], U8, name=name + "_scales", align_bytes=256)
             nc.vector.quantize_mx(
                 out=codes[:].bitcast(FP8X4),
                 scales=scales[:],
                 in_=staged[:].rearrange("p w j -> p (w j)"),
             )
-            for i, block in enumerate(blocks):
-                q_codes[block] = codes[:, i * N_MM : (i + 1) * N_MM]
-                q_scales[block] = scales[:, i * N_MM : (i + 1) * N_MM]
+            return codes, scales
 
-        ns_head = keep.tile([P, 8], F32, name="ns_head")
+        warm = keep.tile([P, 2], F32, name="warm")
+        nc.vector.memset(warm[:, 0:1], 0.0)
         nc.vector.memset(scale_pool[:].bitcast(I32), 0)
-        nc.vector.memset(nb_pool[0:ROW, :], 0.0)
         nc.vector.memset(k_scale[:].bitcast(I32), 0)
+        nc.vector.memset(nb_pool[0:ROW, :], 0.0)
+        nc.vector.memset(ns_pool[0:ROW, :], 0.0)
         make_identity(nc, ident[:])
+        nc.scalar.activation(warm[:, 1:2], warm[:, 0:1], SILU)
 
         nc.sync.dma_start(offsets[:], offs)
-        nc.sync.dma_start(out=ns_head[:], in_=ns[:, 0:8])
         nc.sync.dma_start(out=nb_pool[ROW : ROW + 1, :], in_=nb[0:1, :])
+        nc.sync.dma_start(out=ns_pool[ROW : ROW + 1, :], in_=ns[0:1, :])
         nc.sync.dma_start(
-            out=scale_pool[0 : SCALE_ROWS * SCALE_STEP : SCALE_STEP].bitcast(I32),
+            out=scale_pool[0:P:SCALE_STEP].bitcast(I32),
             in_=k_scales.rearrange("o f t -> f o t").bitcast(I32),
         )
-        nc.sync.dma_start(out=ns_pool[ROW : ROW + 1, :], in_=ns[0:1, :])
-        load_q(0, 0, 256)
+        raw_a0 = load_q(0, 0, 256, 20 * KIB)
         nc.sync.dma_start(out=word_pool[:], in_=k_words[0].rearrange("p t b -> p (t b)").bitcast(I32))
-        load_q(1, 0, 256)
-        load_q(1, 256, 128)
 
-        warm_out = keep.tile([P, 1], F32, name="warm_out")
-        nc.scalar.activation(warm_out[:], ns_head[:, 0:1], SILU)
-        nc.scalar.copy(
-            ns_pool[0:ROW, :].rearrange("p (a b) -> p a b", b=8),
-            ns_head[0:ROW, :].unsqueeze(1).to_broadcast([ROW, T // 8, 8]),
-        )
-        first0 = stage("first0")
-        cast_q(on_scalar, first0, 0, 0, 0, 256, 0)
-        for g in range(PASSES):
-            nc.vector.tensor_copy(scale_listed[:, g, :], scale_pool[:, g, :].indirect(offsets[:]))
-        for r in range(4):
-            rows = scale_listed[SCALE_STEP * r : SCALE_ROWS * SCALE_STEP : 4 * SCALE_STEP]
-            nc.sync.dma_start(out=k_scale[r:P:32].bitcast(I32), in_=rows.bitcast(I32))
-        load_q(0, 256, 256)
-        load_q(1, 384, 128)
+        staged_a0 = stage("staged_a0", 256)
+        cast_q(on_scalar, staged_a0, raw_a0, 0, 256)
 
-        def gather_row(pool, name, tag=None):
-            listed = keep.tile([P, N], F32, name=name + "_listed", align_bytes=64, tag=tag or name + "_listed")
+        nc.vector.tensor_copy(scale_listed[:], scale_pool[:].indirect(offsets[:]))
+        for quad in range(4):
+            nc.sync.dma_start(
+                out=k_scale[32 * quad : 32 * quad + 4].bitcast(I32),
+                in_=scale_listed[32 * quad : 32 * quad + 32 : SCALE_STEP].bitcast(I32),
+            )
+        raw_a1 = load_q(1, 0, 256, 0)
+
+        columns = keep.tile([P, 2, SLOT_TILES], F32, name="columns")
+        nb_cols, ns_cols = columns[:, 0, :], columns[:, 1, :]
+
+        def listed_columns(pool, name, bank, cols):
+            listed = keep.tile([P, N], F32, name=name + "_listed", align_bytes=64)
             nc.vector.tensor_copy(listed[:], pool[:].indirect(offsets[:]))
-            return listed
-
-        def turn(listed, name, bank):
             turned = psum.tile([P, SLOT_TILES, P], F32, name=name + "_turned", tag=bank)
             for j in range(SLOT_TILES):
                 nc.tensor.transpose(turned[:, j, :], listed[:, j * P : (j + 1) * P], ident[:])
-            return turned
+            nc.scalar.copy(cols, turned[:, :, ROW])
 
-        nb_turned = turn(gather_row(nb_pool, "nb"), "nb", "bank4")
-        columns = keep.tile([P, 2, SLOT_TILES], F32, name="columns", tag="raw0_0", align_bytes=256)
-        nb_cols, ns_cols = columns[:, 0, :], columns[:, 1, :]
-        nc.scalar.copy(nb_cols, nb_turned[:, :, ROW])
-        ns_turned = turn(gather_row(ns_pool, "ns"), "ns", "bank5")
-        nc.scalar.copy(ns_cols, ns_turned[:, :, ROW])
-        quantize_q(first0, "first0", [(0, 0), (0, 128)], tag="ns_pool")
+        listed_columns(nb_pool, "nb", "bank4", nb_cols)
+        raw_bc0 = load_q(0, 256, 256, 4 * KIB)
+        listed_columns(ns_pool, "ns", "bank5", ns_cols)
+        raw_b1 = load_q(1, 256, 128, 12 * KIB)
+        raw_c1 = load_q(1, 384, 128, 14 * KIB)
+
+        q_a0 = quantize_q(staged_a0, "a0", 256)
         pairs = keep.tile([P, N], U32, name="pairs")
         nc.vector.tensor_copy(pairs[:], word_pool[:].bitcast(U32).indirect(offsets[:]))
         halves = pairs[:].bitcast(U16).rearrange("p (s h) -> p h s", h=PASSES)
-        k_codes = {}
-
-        def part_words(g, tag):
-            k_codes[g] = keep.tile([P, 2 * N], U8, name=f"k_codes{g}", tag=tag, align_bytes=256)
+        k_codes = []
+        for g in range(PASSES):
+            k_codes.append(keep.tile([P, 2 * N], U8, name=f"k_codes{g}", align_bytes=256))
             nc.vector.tensor_copy(k_codes[g][:].bitcast(U16), halves[:, g, :])
 
-        part_words(0, "k_codes0")
-
-        def multiply(acc, tiles, q0, width, g):
-            sums = [(i, j, n0) for i, j in enumerate(tiles) for n0 in range(0, width, N_MM)]
-            for s, (i, j, n0) in enumerate(sums):
+        def multiply(acc, g, q, c0, width):
+            codes, scales = q
+            for j in range(SLOT_TILES):
                 nc.tensor.matmul_mx(
-                    out=acc[:, i, n0 : n0 + N_MM],
+                    out=acc[j][:],
                     lhsT=k_codes[g][:, 2 * P * j : 2 * P * (j + 1)].bitcast(FP4X4),
                     lhsT_scale=k_scale[:, g, P * j : P * (j + 1)],
-                    rhs=q_codes[g, q0 + n0].bitcast(FP8X4),
-                    rhs_scale=q_scales[g, q0 + n0],
-                    start=(g == 0 and s == 0),
-                    stop=(g == PASSES - 1 and s == len(sums) - 1),
+                    rhs=codes[:, c0 : c0 + width].bitcast(FP8X4),
+                    rhs_scale=scales[:, c0 : c0 + width],
+                    start=(g == 0),
+                    stop=(g == PASSES - 1),
                 )
 
-        def finish(acc, tiles, q0, width, result):
-            for i, j in enumerate(tiles):
-                act = keep.tile([P, width], F32, name=f"act{q0}_{j}")
-                nc.scalar.activation(act[:], acc[:, i, :], SILU, bias=nb_cols[:, j : j + 1])
-                nc.vector.tensor_scalar_mul(result[:, i, :], act[:], ns_cols[:, j : j + 1])
+        def banks(name, first, width):
+            return [psum.tile([P, width], F32, name=f"{name}{j}", tag=f"bank{first + j}") for j in range(SLOT_TILES)]
 
-        def store(result, j0, count, q0, width):
-            rows = out[0, j0 * P : (j0 + count) * P, q0 : q0 + width]
-            nc.sync.dma_start(out=rows.rearrange("(j p) w -> p j w", p=P), in_=result)
-
-        acc_a = [psum.tile([P, 1, 256], F32, name=f"acc_a{j}", tag=f"bank{j}") for j in range(SLOT_TILES)]
-        for j in range(SLOT_TILES):
-            multiply(acc_a[j], [j], 0, 256, 0)
-
-        first1 = stage("first1")
-        cast_q(on_scalar, first1, 0, 1, 0, 256, 0)
-        part_words(1, "k_codes1")
-        quantize_q(first1, "first1", [(1, 0), (1, 128)])
-        second, third = stage("second"), stage("third")
-        cast_q(on_scalar, second, 0, 0, 256, 128, 256)
-        for j in range(SLOT_TILES):
-            multiply(acc_a[j], [j], 0, 256, 1)
-
-        cast_q(on_vector, second, 128, 1, 256, 128, 256)
-        cast_q(on_vector, third, 0, 0, 384, 128, 256)
-        quantize_q(second, "second", [(0, 256), (1, 256)])
-        cast_q(on_vector, third, 128, 1, 384, 128, 384)
-        quantize_q(third, "third", [(0, 384), (1, 384)])
-
-        act_a = keep.tile([P, SLOT_TILES, 256], F32, name="act_a", tag="raw0_256", align_bytes=256)
-        for j in range(SLOT_TILES):
-            nc.scalar.activation(act_a[:, j, :], acc_a[j][:, 0, :], SILU, bias=nb_cols[:, j : j + 1])
-
-        late = {}
-        units = [(256, [0, 1]), (256, [2, 3]), (384, [0, 1]), (384, [2, 3])]
-        for b, (q0, tiles) in enumerate(units):
-            late[b] = psum.tile([P, len(tiles), 128], F32, name=f"late{b}", tag=f"bank{4 + b}")
-            for g in range(PASSES):
-                multiply(late[b], tiles, q0, 128, g)
-
-        early = keep.tile([P, 1, 256], F32, name="early_result", tag="raw1_384", align_bytes=256)
-        rest = keep.tile([P, SLOT_TILES - 1, 256], F32, name="rest_result", tag="third", align_bytes=256)
-        for j in range(SLOT_TILES):
-            result = rest[:, j - 1 : j, :] if j else early[:]
-            nc.vector.tensor_scalar_mul(result[:, 0, :], act_a[:, j, :], ns_cols[:, j : j + 1])
-            store(result, j, 1, 0, 256)
-
-        for b, (q0, tiles) in enumerate(units):
-            groups = [tiles] if b < len(units) - 1 else [[j] for j in tiles]
+        def finish(acc, name, q0, width, groups):
             for group in groups:
-                result = keep.tile([P, len(group), 128], F32, name=f"late_result{q0}_{group[0]}", align_bytes=256)
-                finish(late[b][:, group[0] - tiles[0] :, :], group, q0, 128, result)
-                store(result[:], group[0], len(group), q0, 128)
+                result = keep.tile([P, len(group), width], F32, name=f"{name}_result{group[0]}", align_bytes=256)
+                for i, j in enumerate(group):
+                    act = keep.tile([P, width], F32, name=f"{name}_act{j}")
+                    nc.scalar.activation(act[:], acc[j][:], SILU, bias=nb_cols[:, j : j + 1])
+                    nc.vector.tensor_scalar_mul(result[:, i, :], act[:], ns_cols[:, j : j + 1])
+                rows = out[0, group[0] * P : (group[-1] + 1) * P, q0 : q0 + width]
+                nc.sync.dma_start(out=rows.rearrange("(j p) w -> p j w", p=P), in_=result[:])
+
+        acc_a = banks("acc_a", 0, 256)
+        multiply(acc_a, 0, q_a0, 0, 256)
+
+        staged_a1 = stage("staged_a1", 256)
+        cast_q(on_scalar, staged_a1, raw_a1, 0, 96)
+        cast_q(on_vector, staged_a1, raw_a1, 96, 256)
+        q_a1 = quantize_q(staged_a1, "a1", 256)
+        multiply(acc_a, 1, q_a1, 0, 256)
+
+        staged_bc0 = stage("staged_bc0", 256)
+        cast_q(on_vector, staged_bc0, raw_bc0, 0, 256)
+        q_bc0 = quantize_q(staged_bc0, "bc0", 256)
+        staged_b1 = stage("staged_b1", 128)
+        cast_q(on_vector, staged_b1, raw_b1, 0, 128)
+        q_b1 = quantize_q(staged_b1, "b1", 128)
+        staged_c1 = stage("staged_c1", 128)
+        cast_q(on_vector, staged_c1, raw_c1, 0, 128)
+        q_c1 = quantize_q(staged_c1, "c1", 128)
+
+        finish(acc_a, "a", 0, 256, [[0], [1], [2], [3]])
+
+        acc_b = banks("acc_b", 4, 128)
+        multiply(acc_b, 0, q_bc0, 0, 128)
+        multiply(acc_b, 1, q_b1, 0, 128)
+        acc_c = banks("acc_c", 0, 128)
+        multiply(acc_c, 0, q_bc0, 128, 128)
+        multiply(acc_c, 1, q_c1, 0, 128)
+        finish(acc_b, "b", 256, 128, [[0, 1], [2, 3]])
+        finish(acc_c, "c", 384, 128, [[0, 1], [2], [3]])

@@ -22,7 +22,7 @@ K_PASS = P * PACK
 PASSES = D // K_PASS
 SLOT_TILES = N // P
 ROW = P - 1
-SCALE_STEP = 4
+SCALE_AT = 96
 KIB = 1024
 
 
@@ -57,8 +57,8 @@ def tile_attend_neut_silu_kernel(tc, qT, k_words, k_scales, nb, ns, offs, out):
                 raw[:, :, c0:c1].rearrange("p t (c i) -> p c t i", i=4),
             )
 
-        def stage(name, width):
-            return keep.tile([P, width, PACK], BF16, name=name, align_bytes=256)
+        def stage(name, width, offset):
+            return reuse.tile([P, width, PACK], BF16, name=name, align_bytes=256, offset=offset)
 
         def quantize_q(staged, name, width):
             codes = keep.tile([P, width], U32, name=name + "_codes", align_bytes=256)
@@ -72,7 +72,7 @@ def tile_attend_neut_silu_kernel(tc, qT, k_words, k_scales, nb, ns, offs, out):
 
         warm = keep.tile([P, 2], F32, name="warm")
         nc.vector.memset(warm[:, 0:1], 0.0)
-        nc.vector.memset(scale_pool[:].bitcast(I32), 0)
+        nc.vector.memset(scale_pool[0:SCALE_AT].bitcast(I32), 0)
         nc.vector.memset(k_scale[:].bitcast(I32), 0)
         nc.vector.memset(nb_pool[0:ROW, :], 0.0)
         nc.vector.memset(ns_pool[0:ROW, :], 0.0)
@@ -80,23 +80,23 @@ def tile_attend_neut_silu_kernel(tc, qT, k_words, k_scales, nb, ns, offs, out):
         nc.scalar.activation(warm[:, 1:2], warm[:, 0:1], SILU)
 
         nc.sync.dma_start(offsets[:], offs)
-        nc.sync.dma_start(out=nb_pool[ROW : ROW + 1, :], in_=nb[0:1, :])
-        nc.sync.dma_start(out=ns_pool[ROW : ROW + 1, :], in_=ns[0:1, :])
         nc.sync.dma_start(
-            out=scale_pool[0:P:SCALE_STEP].bitcast(I32),
+            out=scale_pool[SCALE_AT:P].bitcast(I32),
             in_=k_scales.rearrange("o f t -> f o t").bitcast(I32),
         )
+        nc.sync.dma_start(out=nb_pool[ROW : ROW + 1, :], in_=nb[0:1, :])
+        nc.sync.dma_start(out=ns_pool[ROW : ROW + 1, :], in_=ns[0:1, :])
         raw_a0 = load_q(0, 0, 256, 20 * KIB)
         nc.sync.dma_start(out=word_pool[:], in_=k_words[0].rearrange("p t b -> p (t b)").bitcast(I32))
 
-        staged_a0 = stage("staged_a0", 256)
+        staged_a0 = stage("staged_a0", 256, 24 * KIB)
         cast_q(on_scalar, staged_a0, raw_a0, 0, 256)
 
         nc.vector.tensor_copy(scale_listed[:], scale_pool[:].indirect(offsets[:]))
         for quad in range(4):
             nc.sync.dma_start(
                 out=k_scale[32 * quad : 32 * quad + 4].bitcast(I32),
-                in_=scale_listed[32 * quad : 32 * quad + 32 : SCALE_STEP].bitcast(I32),
+                in_=scale_listed[SCALE_AT + 8 * quad : SCALE_AT + 8 * quad + 8].bitcast(I32),
             )
         raw_a1 = load_q(1, 0, 256, 0)
 
@@ -155,23 +155,38 @@ def tile_attend_neut_silu_kernel(tc, qT, k_words, k_scales, nb, ns, offs, out):
         acc_a = banks("acc_a", 0, 256)
         multiply(acc_a, 0, q_a0, 0, 256)
 
-        staged_a1 = stage("staged_a1", 256)
+        staged_a1 = stage("staged_a1", 256, 26 * KIB)
         cast_q(on_scalar, staged_a1, raw_a1, 0, 96)
         cast_q(on_vector, staged_a1, raw_a1, 96, 256)
         q_a1 = quantize_q(staged_a1, "a1", 256)
         multiply(acc_a, 1, q_a1, 0, 256)
 
-        staged_bc0 = stage("staged_bc0", 256)
+        staged_bc0 = stage("staged_bc0", 256, 28 * KIB)
+        staged_b1 = stage("staged_b1", 128, 30 * KIB)
+        staged_c1 = stage("staged_c1", 128, 31 * KIB)
         cast_q(on_vector, staged_bc0, raw_bc0, 0, 256)
-        q_bc0 = quantize_q(staged_bc0, "bc0", 256)
-        staged_b1 = stage("staged_b1", 128)
         cast_q(on_vector, staged_b1, raw_b1, 0, 128)
+        q_bc0 = quantize_q(staged_bc0, "bc0", 256)
         q_b1 = quantize_q(staged_b1, "b1", 128)
-        staged_c1 = stage("staged_c1", 128)
         cast_q(on_vector, staged_c1, raw_c1, 0, 128)
-        q_c1 = quantize_q(staged_c1, "c1", 128)
 
-        finish(acc_a, "a", 0, 256, [[0], [1], [2], [3]])
+        act_a = keep.tile([P, SLOT_TILES, 256], F32, name="act_a")
+        for j in range(SLOT_TILES):
+            nc.scalar.activation(act_a[:, j, :], acc_a[j][:], SILU, bias=nb_cols[:, j : j + 1])
+        result_a = [
+            reuse.tile([P, 2, 256], F32, name=f"result_a{h}", align_bytes=256, offset=offset)
+            for h, offset in enumerate((14 * KIB, 31 * KIB))
+        ]
+
+        def finish_a(j):
+            result = result_a[j // 2][:, j % 2, :]
+            nc.vector.tensor_scalar_mul(result, act_a[:, j, :], ns_cols[:, j : j + 1])
+            nc.sync.dma_start(out=out[0, j * P : (j + 1) * P, 0:256], in_=result)
+
+        finish_a(0)
+        q_c1 = quantize_q(staged_c1, "c1", 128)
+        for j in range(1, SLOT_TILES):
+            finish_a(j)
 
         acc_b = banks("acc_b", 4, 128)
         multiply(acc_b, 0, q_bc0, 0, 128)

@@ -23,6 +23,7 @@ PASSES = D // K_PASS
 SLOT_TILES = N // P
 ROW = P - 1
 SCALE_AT = 96
+HALF = T // 2
 KIB = 1024
 
 
@@ -36,33 +37,33 @@ def tile_attend_neut_silu_kernel(tc, qT, k_words, k_scales, nb, ns, offs, out):
 
         offsets = keep.tile([P, N // 16], U16, name="offsets")
         word_pool = keep.tile([P, T], I32, name="word_pool", align_bytes=256)
-        scale_pool = reuse.tile([P, T], U8, name="scale_pool", align_bytes=256, offset=0)
-        nb_pool = reuse.tile([P, T], F32, name="nb_pool", align_bytes=256, offset=4 * KIB)
-        ns_pool = reuse.tile([P, T], F32, name="ns_pool", align_bytes=256, offset=12 * KIB)
-        ident = keep.tile([P, P], F32, name="ident")
         scale_listed = keep.tile([P, N], U8, name="scale_listed", align_bytes=256)
         k_scale = keep.tile([P, PASSES, N], U8, name="k_scale", align_bytes=256)
 
-        def load_q(g, q0, width, offset):
-            raw = reuse.tile([P, PACK, width], F32, name=f"raw{g}_{q0}", align_bytes=256, offset=offset)
+        def placed(name, shape, dtype, kib):
+            return reuse.tile(shape, dtype, name=name, align_bytes=256, offset=kib * KIB)
+
+        scale_pool = placed("scale_pool", [P, T], U8, 3)
+        nb_pool = placed("nb_pool", [P, T], F32, 8)
+        ns_pool = placed("ns_pool", [P, T], F32, 16)
+
+        def load_q(g, q0, width, kib):
+            raw = placed(f"raw{g}_{q0}", [P, PACK, width], F32, kib)
             rows = qT[0, g * K_PASS : (g + 1) * K_PASS, q0 : q0 + width]
             nc.sync.dma_start(out=raw[:], in_=rows.rearrange("(p j) w -> p j w", j=PACK))
             return raw
 
         on_scalar, on_vector = nc.scalar.copy, nc.vector.tensor_copy
 
-        def cast_q(copy, staged, raw, c0, c1):
+        def cast_q(copy, staged, at, raw, c0, c1):
             copy(
-                staged[:, c0:c1, :].rearrange("p (c i) t -> p c t i", i=4),
+                staged[:, at + c0 : at + c1, :].rearrange("p (c i) t -> p c t i", i=4),
                 raw[:, :, c0:c1].rearrange("p t (c i) -> p c t i", i=4),
             )
 
-        def stage(name, width, offset):
-            return reuse.tile([P, width, PACK], BF16, name=name, align_bytes=256, offset=offset)
-
-        def quantize_q(staged, name, width):
-            codes = keep.tile([P, width], U32, name=name + "_codes", align_bytes=256)
-            scales = keep.tile([P, width], U8, name=name + "_scales", align_bytes=256)
+        def quantize_q(staged, name):
+            codes = keep.tile([P, 256], U32, name=name + "_codes", align_bytes=256)
+            scales = keep.tile([P, 256], U8, name=name + "_scales", align_bytes=256)
             nc.vector.quantize_mx(
                 out=codes[:].bitcast(FP8X4),
                 scales=scales[:],
@@ -75,22 +76,21 @@ def tile_attend_neut_silu_kernel(tc, qT, k_words, k_scales, nb, ns, offs, out):
         nc.vector.memset(scale_pool[0:SCALE_AT].bitcast(I32), 0)
         nc.vector.memset(k_scale[:].bitcast(I32), 0)
         nc.vector.memset(nb_pool[0:ROW, :], 0.0)
-        nc.vector.memset(ns_pool[0:ROW, :], 0.0)
-        make_identity(nc, ident[:])
+        nc.vector.memset(ns_pool[0:ROW, 0:HALF], 0.0)
         nc.scalar.activation(warm[:, 1:2], warm[:, 0:1], SILU)
 
-        nc.sync.dma_start(offsets[:], offs)
         nc.sync.dma_start(
             out=scale_pool[SCALE_AT:P].bitcast(I32),
             in_=k_scales.rearrange("o f t -> f o t").bitcast(I32),
         )
+        nc.sync.dma_start(offsets[:], offs)
         nc.sync.dma_start(out=nb_pool[ROW : ROW + 1, :], in_=nb[0:1, :])
         nc.sync.dma_start(out=ns_pool[ROW : ROW + 1, :], in_=ns[0:1, :])
-        raw_a0 = load_q(0, 0, 256, 20 * KIB)
+        raw_a0 = load_q(0, 0, 256, 24)
         nc.sync.dma_start(out=word_pool[:], in_=k_words[0].rearrange("p t b -> p (t b)").bitcast(I32))
 
-        staged_a0 = stage("staged_a0", 256, 24 * KIB)
-        cast_q(on_scalar, staged_a0, raw_a0, 0, 256)
+        staged_a0 = placed("staged_a0", [P, 256, PACK], BF16, 28)
+        cast_q(on_scalar, staged_a0, 0, raw_a0, 0, 256)
 
         nc.vector.tensor_copy(scale_listed[:], scale_pool[:].indirect(offsets[:]))
         for quad in range(4):
@@ -99,8 +99,11 @@ def tile_attend_neut_silu_kernel(tc, qT, k_words, k_scales, nb, ns, offs, out):
                 in_=scale_listed[SCALE_AT + 8 * quad : SCALE_AT + 8 * quad + 8].bitcast(I32),
             )
         raw_a1 = load_q(1, 0, 256, 0)
+        ident = placed("ident", [P, P], F32, 4)
+        make_identity(nc, ident[:])
+        nc.vector.memset(ns_pool[0:ROW, HALF:T], 0.0)
 
-        columns = keep.tile([P, 2, SLOT_TILES], F32, name="columns")
+        columns = placed("columns", [P, 2, SLOT_TILES], F32, 24)
         nb_cols, ns_cols = columns[:, 0, :], columns[:, 1, :]
 
         def listed_columns(pool, name, bank, cols):
@@ -112,12 +115,13 @@ def tile_attend_neut_silu_kernel(tc, qT, k_words, k_scales, nb, ns, offs, out):
             nc.scalar.copy(cols, turned[:, :, ROW])
 
         listed_columns(nb_pool, "nb", "bank4", nb_cols)
-        raw_bc0 = load_q(0, 256, 256, 4 * KIB)
+        raw_b0 = load_q(0, 256, 128, 8)
+        raw_b1 = load_q(1, 256, 128, 10)
         listed_columns(ns_pool, "ns", "bank5", ns_cols)
-        raw_b1 = load_q(1, 256, 128, 12 * KIB)
-        raw_c1 = load_q(1, 384, 128, 14 * KIB)
+        raw_c0 = load_q(0, 384, 128, 16)
+        raw_c1 = load_q(1, 384, 128, 18)
 
-        q_a0 = quantize_q(staged_a0, "a0", 256)
+        q_a0 = quantize_q(staged_a0, "a0")
         pairs = keep.tile([P, N], U32, name="pairs")
         nc.vector.tensor_copy(pairs[:], word_pool[:].bitcast(U32).indirect(offsets[:]))
         halves = pairs[:].bitcast(U16).rearrange("p (s h) -> p h s", h=PASSES)
@@ -126,73 +130,72 @@ def tile_attend_neut_silu_kernel(tc, qT, k_words, k_scales, nb, ns, offs, out):
             k_codes.append(keep.tile([P, 2 * N], U8, name=f"k_codes{g}", align_bytes=256))
             nc.vector.tensor_copy(k_codes[g][:].bitcast(U16), halves[:, g, :])
 
-        def multiply(acc, g, q, c0, width):
+        def one_pass(acc, j, g, q, c0, width):
             codes, scales = q
-            for j in range(SLOT_TILES):
-                nc.tensor.matmul_mx(
-                    out=acc[j][:],
-                    lhsT=k_codes[g][:, 2 * P * j : 2 * P * (j + 1)].bitcast(FP4X4),
-                    lhsT_scale=k_scale[:, g, P * j : P * (j + 1)],
-                    rhs=codes[:, c0 : c0 + width].bitcast(FP8X4),
-                    rhs_scale=scales[:, c0 : c0 + width],
-                    start=(g == 0),
-                    stop=(g == PASSES - 1),
-                )
+            nc.tensor.matmul_mx(
+                out=acc[j][:],
+                lhsT=k_codes[g][:, 2 * P * j : 2 * P * (j + 1)].bitcast(FP4X4),
+                lhsT_scale=k_scale[:, g, P * j : P * (j + 1)],
+                rhs=codes[:, c0 : c0 + width].bitcast(FP8X4),
+                rhs_scale=scales[:, c0 : c0 + width],
+                start=(g == 0),
+                stop=(g == PASSES - 1),
+            )
 
         def banks(name, first, width):
             return [psum.tile([P, width], F32, name=f"{name}{j}", tag=f"bank{first + j}") for j in range(SLOT_TILES)]
 
-        def finish(acc, name, q0, width, groups):
-            for group in groups:
-                result = keep.tile([P, len(group), width], F32, name=f"{name}_result{group[0]}", align_bytes=256)
-                for i, j in enumerate(group):
-                    act = keep.tile([P, width], F32, name=f"{name}_act{j}")
-                    nc.scalar.activation(act[:], acc[j][:], SILU, bias=nb_cols[:, j : j + 1])
-                    nc.vector.tensor_scalar_mul(result[:, i, :], act[:], ns_cols[:, j : j + 1])
-                rows = out[0, group[0] * P : (group[-1] + 1) * P, q0 : q0 + width]
-                nc.sync.dma_start(out=rows.rearrange("(j p) w -> p j w", p=P), in_=result[:])
+        def multiply_late(name, first, q):
+            acc = banks(name, first, 128)
+            for j in range(SLOT_TILES):
+                for g in range(PASSES):
+                    one_pass(acc, j, g, q, 128 * g, 128)
+            return acc
+
+        def activate(act, acc):
+            for j in range(SLOT_TILES):
+                nc.scalar.activation(act[:, j, :], acc[j][:], SILU, bias=nb_cols[:, j : j + 1])
+
+        def finish(result, act, j0, j1, q0):
+            for j in range(j0, j1):
+                nc.vector.tensor_scalar_mul(result[:, j - j0, :], act[:, j, :], ns_cols[:, j : j + 1])
+            rows = out[0, j0 * P : j1 * P, q0 : q0 + result.shape[2]]
+            nc.sync.dma_start(out=rows.rearrange("(j p) w -> p j w", p=P), in_=result[:])
 
         acc_a = banks("acc_a", 0, 256)
-        multiply(acc_a, 0, q_a0, 0, 256)
-
-        staged_a1 = stage("staged_a1", 256, 26 * KIB)
-        cast_q(on_scalar, staged_a1, raw_a1, 0, 96)
-        cast_q(on_vector, staged_a1, raw_a1, 96, 256)
-        q_a1 = quantize_q(staged_a1, "a1", 256)
-        multiply(acc_a, 1, q_a1, 0, 256)
-
-        staged_bc0 = stage("staged_bc0", 256, 28 * KIB)
-        staged_b1 = stage("staged_b1", 128, 30 * KIB)
-        staged_c1 = stage("staged_c1", 128, 31 * KIB)
-        cast_q(on_vector, staged_bc0, raw_bc0, 0, 256)
-        cast_q(on_vector, staged_b1, raw_b1, 0, 128)
-        q_bc0 = quantize_q(staged_bc0, "bc0", 256)
-        q_b1 = quantize_q(staged_b1, "b1", 128)
-        cast_q(on_vector, staged_c1, raw_c1, 0, 128)
-
-        act_a = keep.tile([P, SLOT_TILES, 256], F32, name="act_a")
         for j in range(SLOT_TILES):
-            nc.scalar.activation(act_a[:, j, :], acc_a[j][:], SILU, bias=nb_cols[:, j : j + 1])
-        result_a = [
-            reuse.tile([P, 2, 256], F32, name=f"result_a{h}", align_bytes=256, offset=offset)
-            for h, offset in enumerate((14 * KIB, 31 * KIB))
-        ]
+            one_pass(acc_a, j, 0, q_a0, 0, 256)
 
-        def finish_a(j):
-            result = result_a[j // 2][:, j % 2, :]
-            nc.vector.tensor_scalar_mul(result, act_a[:, j, :], ns_cols[:, j : j + 1])
-            nc.sync.dma_start(out=out[0, j * P : (j + 1) * P, 0:256], in_=result)
+        staged_a1 = placed("staged_a1", [P, 256, PACK], BF16, 30)
+        cast_q(on_scalar, staged_a1, 0, raw_a1, 0, 96)
+        cast_q(on_vector, staged_a1, 0, raw_a1, 96, 256)
+        q_a1 = quantize_q(staged_a1, "a1")
+        for j in range(SLOT_TILES):
+            one_pass(acc_a, j, 1, q_a1, 0, 256)
 
-        finish_a(0)
-        q_c1 = quantize_q(staged_c1, "c1", 128)
-        for j in range(1, SLOT_TILES):
-            finish_a(j)
+        staged_b = placed("staged_b", [P, 256, PACK], BF16, 32)
+        staged_c = placed("staged_c", [P, 256, PACK], BF16, 34)
+        cast_q(on_scalar, staged_b, 0, raw_b0, 0, 128)
+        act_a = placed("act_a", [P, SLOT_TILES, 256], F32, 6)
+        activate(act_a, acc_a)
+        cast_q(on_vector, staged_b, 128, raw_b1, 0, 128)
+        q_b = quantize_q(staged_b, "b")
+        acc_b = multiply_late("acc_b", 4, q_b)
+        cast_q(on_vector, staged_c, 0, raw_c0, 0, 128)
+        finish(placed("result_a0", [P, 1, 256], F32, 32), act_a, 0, 1, 0)
+        cast_q(on_vector, staged_c, 128, raw_c1, 0, 128)
+        finish(placed("result_a1", [P, 1, 256], F32, 16), act_a, 1, 2, 0)
+        q_c = quantize_q(staged_c, "c")
+        acc_c = multiply_late("acc_c", 0, q_c)
+        finish(placed("result_a2", [P, 1, 256], F32, 18), act_a, 2, 3, 0)
+        finish(placed("result_a3", [P, 1, 256], F32, 19), act_a, 3, 4, 0)
 
-        acc_b = banks("acc_b", 4, 128)
-        multiply(acc_b, 0, q_bc0, 0, 128)
-        multiply(acc_b, 1, q_b1, 0, 128)
-        acc_c = banks("acc_c", 0, 128)
-        multiply(acc_c, 0, q_bc0, 128, 128)
-        multiply(acc_c, 1, q_c1, 0, 128)
-        finish(acc_b, "b", 256, 128, [[0, 1], [2, 3]])
-        finish(acc_c, "c", 384, 128, [[0, 1], [2], [3]])
+        act_b = placed("act_b", [P, SLOT_TILES, 128], F32, 36)
+        activate(act_b, acc_b)
+        finish(placed("result_b0", [P, 2, 128], F32, 34), act_b, 0, 2, 256)
+        finish(placed("result_b2", [P, 2, 128], F32, 35), act_b, 2, 4, 256)
+        act_c = placed("act_c", [P, SLOT_TILES, 128], F32, 38)
+        activate(act_c, acc_c)
+        finish(placed("result_c0", [P, 2, 128], F32, 40), act_c, 0, 2, 384)
+        finish(placed("result_c2", [P, 1, 128], F32, 41), act_c, 2, 3, 384)
+        finish(placed("result_c3", [P, 1, 128], F32, 42), act_c, 3, 4, 384)

@@ -22,7 +22,7 @@ K_PASS = P * PACK
 PASSES = D // K_PASS
 SLOT_TILES = N // P
 ROW = P - 1
-SCALE_AT = 96
+SCALE_AT = 32
 HALF = T // 2
 KIB = 1024
 
@@ -74,13 +74,14 @@ def tile_attend_neut_silu_kernel(tc, qT, k_words, k_scales, nb, ns, offs, out):
         warm = keep.tile([P, 2], F32, name="warm")
         nc.vector.memset(warm[:, 0:1], 0.0)
         nc.vector.memset(scale_pool[0:SCALE_AT].bitcast(I32), 0)
+        nc.vector.memset(scale_pool[2 * SCALE_AT : P].bitcast(I32), 0)
         nc.vector.memset(k_scale[:].bitcast(I32), 0)
         nc.vector.memset(nb_pool[0:ROW, :], 0.0)
         nc.vector.memset(ns_pool[0:ROW, 0:HALF], 0.0)
         nc.scalar.activation(warm[:, 1:2], warm[:, 0:1], SILU)
 
         nc.sync.dma_start(
-            out=scale_pool[SCALE_AT:P].bitcast(I32),
+            out=scale_pool[SCALE_AT : 2 * SCALE_AT].bitcast(I32),
             in_=k_scales.rearrange("o f t -> f o t").bitcast(I32),
         )
         nc.sync.dma_start(offsets[:], offs)
@@ -93,7 +94,7 @@ def tile_attend_neut_silu_kernel(tc, qT, k_words, k_scales, nb, ns, offs, out):
         cast_q(on_scalar, staged_a0, 0, raw_a0, 0, 256)
 
         nc.vector.tensor_copy(scale_listed[:], scale_pool[:].indirect(offsets[:]))
-        for quad in range(4):
+        for quad in (0, 2, 1, 3):
             nc.sync.dma_start(
                 out=k_scale[32 * quad : 32 * quad + 4].bitcast(I32),
                 in_=scale_listed[SCALE_AT + 8 * quad : SCALE_AT + 8 * quad + 8].bitcast(I32),

@@ -15,6 +15,7 @@ U8 = mybir.dt.uint8
 FP8X4 = mybir.dt.float8_e4m3fn_x4
 FP4X4 = mybir.dt.float4_e2m1fn_x4
 SILU = mybir.ActivationFunctionType.Silu
+COPY = mybir.ActivationFunctionType.Copy
 
 P = 128
 PACK = 4
@@ -73,11 +74,11 @@ def tile_attend_neut_silu_kernel(tc, qT, k_words, k_scales, nb, ns, offs, out):
 
         warm = keep.tile([P, 2], F32, name="warm")
         nc.vector.memset(warm[:, 0:1], 0.0)
+        nc.vector.memset(ns_pool[0:ROW, :], 0.0)
         nc.vector.memset(scale_pool[0:SCALE_AT].bitcast(I32), 0)
         nc.vector.memset(scale_pool[2 * SCALE_AT : P].bitcast(I32), 0)
         nc.vector.memset(k_scale[:].bitcast(I32), 0)
-        nc.vector.memset(nb_pool[0:ROW, :], 0.0)
-        nc.vector.memset(ns_pool[0:ROW, 0:HALF], 0.0)
+        nc.vector.memset(nb_pool[0:ROW, 0:HALF], 0.0)
         nc.scalar.activation(warm[:, 1:2], warm[:, 0:1], SILU)
 
         nc.sync.dma_start(
@@ -85,8 +86,10 @@ def tile_attend_neut_silu_kernel(tc, qT, k_words, k_scales, nb, ns, offs, out):
             in_=k_scales.rearrange("o f t -> f o t").bitcast(I32),
         )
         nc.sync.dma_start(offsets[:], offs)
-        nc.sync.dma_start(out=nb_pool[ROW : ROW + 1, :], in_=nb[0:1, :])
         nc.sync.dma_start(out=ns_pool[ROW : ROW + 1, :], in_=ns[0:1, :])
+        nc.sync.dma_start(out=nb_pool[ROW : ROW + 1, :], in_=nb[0:1, :])
+        ns_listed = keep.tile([P, N], F32, name="ns_listed", align_bytes=64)
+        nc.scalar.activation(ns_listed[:], ns_pool[:].indirect(offsets[:]), COPY)
         raw_a0 = load_q(0, 0, 256, 24)
         nc.sync.dma_start(out=word_pool[:], in_=k_words[0].rearrange("p t b -> p (t b)").bitcast(I32))
 
@@ -102,23 +105,23 @@ def tile_attend_neut_silu_kernel(tc, qT, k_words, k_scales, nb, ns, offs, out):
         raw_a1 = load_q(1, 0, 256, 0)
         ident = placed("ident", [P, P], F32, 4)
         make_identity(nc, ident[:])
-        nc.vector.memset(ns_pool[0:ROW, HALF:T], 0.0)
+        nc.vector.memset(nb_pool[0:ROW, HALF:T], 0.0)
 
         columns = placed("columns", [P, 2, SLOT_TILES], F32, 24)
         nb_cols, ns_cols = columns[:, 0, :], columns[:, 1, :]
 
-        def listed_columns(pool, name, bank, cols):
-            listed = keep.tile([P, N], F32, name=name + "_listed", align_bytes=64)
-            nc.vector.tensor_copy(listed[:], pool[:].indirect(offsets[:]))
+        def turn_to_columns(listed, name, bank, cols):
             turned = psum.tile([P, SLOT_TILES, P], F32, name=name + "_turned", tag=bank)
             for j in range(SLOT_TILES):
                 nc.tensor.transpose(turned[:, j, :], listed[:, j * P : (j + 1) * P], ident[:])
             nc.scalar.copy(cols, turned[:, :, ROW])
 
-        listed_columns(nb_pool, "nb", "bank4", nb_cols)
+        nb_listed = keep.tile([P, N], F32, name="nb_listed", align_bytes=64)
+        nc.vector.tensor_copy(nb_listed[:], nb_pool[:].indirect(offsets[:]))
+        turn_to_columns(nb_listed, "nb", "bank4", nb_cols)
         raw_b0 = load_q(0, 256, 128, 8)
         raw_b1 = load_q(1, 256, 128, 10)
-        listed_columns(ns_pool, "ns", "bank5", ns_cols)
+        turn_to_columns(ns_listed, "ns", "bank5", ns_cols)
         raw_c0 = load_q(0, 384, 128, 16)
         raw_c1 = load_q(1, 384, 128, 18)
 

@@ -23,8 +23,7 @@ K_PASS = P * PACK
 PASSES = D // K_PASS
 SLOT_TILES = N // P
 ROW = P - 1
-SCALE_AT = 32
-HALF = T // 2
+SCALE_AT = 96
 KIB = 1024
 
 
@@ -74,24 +73,22 @@ def tile_attend_neut_silu_kernel(tc, qT, k_words, k_scales, nb, ns, offs, out):
 
         warm = keep.tile([P, 2], F32, name="warm")
         nc.vector.memset(warm[:, 0:1], 0.0)
-        nc.vector.memset(ns_pool[0:ROW, :], 0.0)
         nc.vector.memset(scale_pool[0:SCALE_AT].bitcast(I32), 0)
-        nc.vector.memset(scale_pool[2 * SCALE_AT : P].bitcast(I32), 0)
         nc.vector.memset(k_scale[:].bitcast(I32), 0)
-        nc.vector.memset(nb_pool[0:ROW, 0:HALF], 0.0)
+        nc.vector.memset(nb_pool[0:ROW, :], 0.0)
+        nc.vector.memset(ns_pool[0:ROW, :], 0.0)
         nc.scalar.activation(warm[:, 1:2], warm[:, 0:1], SILU)
 
+        raw_a0 = load_q(0, 0, 256, 24)
         nc.sync.dma_start(
-            out=scale_pool[SCALE_AT : 2 * SCALE_AT].bitcast(I32),
+            out=scale_pool[SCALE_AT:P].bitcast(I32),
             in_=k_scales.rearrange("o f t -> f o t").bitcast(I32),
         )
         nc.sync.dma_start(offsets[:], offs)
-        nc.sync.dma_start(out=ns_pool[ROW : ROW + 1, :], in_=ns[0:1, :])
         nc.sync.dma_start(out=nb_pool[ROW : ROW + 1, :], in_=nb[0:1, :])
-        ns_listed = keep.tile([P, N], F32, name="ns_listed", align_bytes=64)
-        nc.scalar.activation(ns_listed[:], ns_pool[:].indirect(offsets[:]), COPY)
-        raw_a0 = load_q(0, 0, 256, 24)
+        nc.sync.dma_start(out=ns_pool[ROW : ROW + 1, :], in_=ns[0:1, :])
         nc.sync.dma_start(out=word_pool[:], in_=k_words[0].rearrange("p t b -> p (t b)").bitcast(I32))
+        raw_a1 = load_q(1, 0, 256, 44)
 
         staged_a0 = placed("staged_a0", [P, 256, PACK], BF16, 28)
         cast_q(on_scalar, staged_a0, 0, raw_a0, 0, 256)
@@ -102,26 +99,24 @@ def tile_attend_neut_silu_kernel(tc, qT, k_words, k_scales, nb, ns, offs, out):
                 out=k_scale[32 * quad : 32 * quad + 4].bitcast(I32),
                 in_=scale_listed[SCALE_AT + 8 * quad : SCALE_AT + 8 * quad + 8].bitcast(I32),
             )
-        raw_a1 = load_q(1, 0, 256, 0)
-        ident = placed("ident", [P, P], F32, 4)
+        raw_b0 = load_q(0, 256, 128, 4)
+        ident = placed("ident", [P, P], F32, 3)
         make_identity(nc, ident[:])
-        nc.vector.memset(nb_pool[0:ROW, HALF:T], 0.0)
 
         columns = placed("columns", [P, 2, SLOT_TILES], F32, 24)
         nb_cols, ns_cols = columns[:, 0, :], columns[:, 1, :]
 
-        def turn_to_columns(listed, name, bank, cols):
+        def listed_columns(pool, name, bank, cols):
+            listed = keep.tile([P, N], F32, name=name + "_listed", align_bytes=64)
+            nc.scalar.activation(listed[:], pool[:].indirect(offsets[:]), COPY)
             turned = psum.tile([P, SLOT_TILES, P], F32, name=name + "_turned", tag=bank)
             for j in range(SLOT_TILES):
                 nc.tensor.transpose(turned[:, j, :], listed[:, j * P : (j + 1) * P], ident[:])
             nc.scalar.copy(cols, turned[:, :, ROW])
 
-        nb_listed = keep.tile([P, N], F32, name="nb_listed", align_bytes=64)
-        nc.vector.tensor_copy(nb_listed[:], nb_pool[:].indirect(offsets[:]))
-        turn_to_columns(nb_listed, "nb", "bank4", nb_cols)
-        raw_b0 = load_q(0, 256, 128, 8)
+        listed_columns(nb_pool, "nb", "bank4", nb_cols)
         raw_b1 = load_q(1, 256, 128, 10)
-        turn_to_columns(ns_listed, "ns", "bank5", ns_cols)
+        listed_columns(ns_pool, "ns", "bank5", ns_cols)
         raw_c0 = load_q(0, 384, 128, 16)
         raw_c1 = load_q(1, 384, 128, 18)
 
@@ -171,8 +166,8 @@ def tile_attend_neut_silu_kernel(tc, qT, k_words, k_scales, nb, ns, offs, out):
             one_pass(acc_a, j, 0, q_a0, 0, 256)
 
         staged_a1 = placed("staged_a1", [P, 256, PACK], BF16, 30)
-        cast_q(on_scalar, staged_a1, 0, raw_a1, 0, 96)
-        cast_q(on_vector, staged_a1, 0, raw_a1, 96, 256)
+        cast_q(on_scalar, staged_a1, 0, raw_a1, 0, 128)
+        cast_q(on_vector, staged_a1, 0, raw_a1, 128, 256)
         q_a1 = quantize_q(staged_a1, "a1")
         for j in range(SLOT_TILES):
             one_pass(acc_a, j, 1, q_a1, 0, 256)
@@ -180,7 +175,7 @@ def tile_attend_neut_silu_kernel(tc, qT, k_words, k_scales, nb, ns, offs, out):
         staged_b = placed("staged_b", [P, 256, PACK], BF16, 32)
         staged_c = placed("staged_c", [P, 256, PACK], BF16, 34)
         cast_q(on_scalar, staged_b, 0, raw_b0, 0, 128)
-        act_a = placed("act_a", [P, SLOT_TILES, 256], F32, 6)
+        act_a = placed("act_a", [P, SLOT_TILES, 256], F32, 5)
         activate(act_a, acc_a)
         cast_q(on_vector, staged_b, 128, raw_b1, 0, 128)
         q_b = quantize_q(staged_b, "b")

from contextlib import ExitStack

import concourse.mybir as mybir
from concourse.masks import make_identity

N, T, D, NQ = 512, 2048, 1024, 512
FLOPS = 2 * N * D * NQ

F32 = mybir.dt.float32
BF16 = mybir.dt.bfloat16
I32 = mybir.dt.int32
U32 = mybir.dt.uint32
U16 = mybir.dt.uint16
U8 = mybir.dt.uint8
FP8X4 = mybir.dt.float8_e4m3fn_x4
FP4X4 = mybir.dt.float4_e2m1fn_x4
SILU = mybir.ActivationFunctionType.Silu
COPY = mybir.ActivationFunctionType.Copy

P = 128
PACK = 4
K_PASS = P * PACK
PASSES = D // K_PASS
SLOT_TILES = N // P
ROW = P - 1
SCALE_AT = 96
KIB = 1024


def tile_attend_neut_silu_kernel(tc, qT, k_words, k_scales, nb, ns, offs, out):
    nc = tc.nc

    with ExitStack() as ctx:
        keep = ctx.enter_context(tc.tile_pool(name="keep", bufs=1))
        reuse = ctx.enter_context(tc.tile_pool(name="reuse", bufs=1))
        psum = ctx.enter_context(tc.psum_pool(name="psum", bufs=1))

        offsets = keep.tile([P, N // 16], U16, name="offsets")
        word_pool = keep.tile([P, T], I32, name="word_pool", align_bytes=256)
        scale_listed = keep.tile([P, N], U8, name="scale_listed", align_bytes=256)
        k_scale = keep.tile([P, PASSES, N], U8, name="k_scale", align_bytes=256)

        def placed(name, shape, dtype, kib):
            return reuse.tile(shape, dtype, name=name, align_bytes=256, offset=kib * KIB)

        scale_pool = placed("scale_pool", [P, T], U8, 3)
        nb_pool = placed("nb_pool", [P, T], F32, 8)
        ns_pool = placed("ns_pool", [P, T], F32, 16)

        def load_q(g, q0, width, kib):
            raw = placed(f"raw{g}_{q0}", [P, PACK, width], F32, kib)
            rows = qT[0, g * K_PASS : (g + 1) * K_PASS, q0 : q0 + width]
            nc.sync.dma_start(out=raw[:], in_=rows.rearrange("(p j) w -> p j w", j=PACK))
            return raw

        on_scalar, on_vector = nc.scalar.copy, nc.vector.tensor_copy

        def cast_q(copy, staged, at, raw, c0, c1):
            copy(
                staged[:, at + c0 : at + c1, :].rearrange("p (c i) t -> p c t i", i=4),
                raw[:, :, c0:c1].rearrange("p t (c i) -> p c t i", i=4),
            )

        def quantize_q(staged, name):
            codes = keep.tile([P, 256], U32, name=name + "_codes", align_bytes=256)
            scales = keep.tile([P, 256], U8, name=name + "_scales", align_bytes=256)
            nc.vector.quantize_mx(
                out=codes[:].bitcast(FP8X4),
                scales=scales[:],
                in_=staged[:].rearrange("p w j -> p (w j)"),
            )
            return codes, scales

        warm = keep.tile([P, 2], F32, name="warm")
        nc.vector.memset(warm[:, 0:1], 0.0)
        nc.vector.memset(scale_pool[0:SCALE_AT].bitcast(I32), 0)
        nc.vector.memset(k_scale[:].bitcast(I32), 0)
        nc.vector.memset(nb_pool[0:ROW, :], 0.0)
        nc.vector.memset(ns_pool[0:ROW, :], 0.0)
        nc.scalar.activation(warm[:, 1:2], warm[:, 0:1], SILU)

        raw_a0 = load_q(0, 0, 256, 24)
        nc.sync.dma_start(
            out=scale_pool[SCALE_AT:P].bitcast(I32),
            in_=k_scales.rearrange("o f t -> f o t").bitcast(I32),
        )
        nc.sync.dma_start(offsets[:], offs)
        nc.sync.dma_start(out=nb_pool[ROW : ROW + 1, :], in_=nb[0:1, :])
        nc.sync.dma_start(out=ns_pool[ROW : ROW + 1, :], in_=ns[0:1, :])
        nc.sync.dma_start(out=word_pool[:], in_=k_words[0].rearrange("p t b -> p (t b)").bitcast(I32))
        raw_a1 = load_q(1, 0, 256, 44)

        staged_a0 = placed("staged_a0", [P, 256, PACK], BF16, 28)
        cast_q(on_scalar, staged_a0, 0, raw_a0, 0, 256)

        nc.vector.tensor_copy(scale_listed[:], scale_pool[:].indirect(offsets[:]))
        for quad in (0, 2, 1, 3):
            nc.sync.dma_start(
                out=k_scale[32 * quad : 32 * quad + 4].bitcast(I32),
                in_=scale_listed[SCALE_AT + 8 * quad : SCALE_AT + 8 * quad + 8].bitcast(I32),
            )
        raw_b0 = load_q(0, 256, 128, 4)
        ident = placed("ident", [P, P], F32, 3)
        make_identity(nc, ident[:])

        columns = placed("columns", [P, 2, SLOT_TILES], F32, 24)
        nb_cols, ns_cols = columns[:, 0, :], columns[:, 1, :]

        def listed_columns(pool, name, bank, cols):
            listed = keep.tile([P, N], F32, name=name + "_listed", align_bytes=64)
            nc.scalar.activation(listed[:], pool[:].indirect(offsets[:]), COPY)
            turned = psum.tile([P, SLOT_TILES, P], F32, name=name + "_turned", tag=bank)
            for j in range(SLOT_TILES):
                nc.tensor.transpose(turned[:, j, :], listed[:, j * P : (j + 1) * P], ident[:])
            nc.scalar.copy(cols, turned[:, :, ROW])

        listed_columns(nb_pool, "nb", "bank4", nb_cols)
        raw_b1 = load_q(1, 256, 128, 10)
        listed_columns(ns_pool, "ns", "bank5", ns_cols)
        raw_c0 = load_q(0, 384, 128, 16)
        raw_c1 = load_q(1, 384, 128, 18)

        q_a0 = quantize_q(staged_a0, "a0")
        pairs = keep.tile([P, N], U32, name="pairs")
        nc.vector.tensor_copy(pairs[:], word_pool[:].bitcast(U32).indirect(offsets[:]))
        halves = pairs[:].bitcast(U16).rearrange("p (s h) -> p h s", h=PASSES)
        k_codes = []
        for g in range(PASSES):
            k_codes.append(keep.tile([P, 2 * N], U8, name=f"k_codes{g}", align_bytes=256))
            nc.vector.tensor_copy(k_codes[g][:].bitcast(U16), halves[:, g, :])

        def one_pass(acc, j, g, q, c0, width):
            codes, scales = q
            nc.tensor.matmul_mx(
                out=acc[j][:],
                lhsT=k_codes[g][:, 2 * P * j : 2 * P * (j + 1)].bitcast(FP4X4),
                lhsT_scale=k_scale[:, g, P * j : P * (j + 1)],
                rhs=codes[:, c0 : c0 + width].bitcast(FP8X4),
                rhs_scale=scales[:, c0 : c0 + width],
                start=(g == 0),
                stop=(g == PASSES - 1),
            )

        def banks(name, first, width):
            return [psum.tile([P, width], F32, name=f"{name}{j}", tag=f"bank{first + j}") for j in range(SLOT_TILES)]

        def multiply_late(name, first, q):
            acc = banks(name, first, 128)
            for j in range(SLOT_TILES):
                for g in range(PASSES):
                    one_pass(acc, j, g, q, 128 * g, 128)
            return acc

        def activate(act, acc):
            for j in range(SLOT_TILES):
                nc.scalar.activation(act[:, j, :], acc[j][:], SILU, bias=nb_cols[:, j : j + 1])

        def finish(result, act, j0, j1, q0):
            for j in range(j0, j1):
                nc.vector.tensor_scalar_mul(result[:, j - j0, :], act[:, j, :], ns_cols[:, j : j + 1])
            rows = out[0, j0 * P : j1 * P, q0 : q0 + result.shape[2]]
            nc.sync.dma_start(out=rows.rearrange("(j p) w -> p j w", p=P), in_=result[:])

        acc_a = banks("acc_a", 0, 256)
        for j in range(SLOT_TILES):
            one_pass(acc_a, j, 0, q_a0, 0, 256)

        staged_a1 = placed("staged_a1", [P, 256, PACK], BF16, 30)
        cast_q(on_scalar, staged_a1, 0, raw_a1, 0, 128)
        cast_q(on_vector, staged_a1, 0, raw_a1, 128, 256)
        q_a1 = quantize_q(staged_a1, "a1")
        for j in range(SLOT_TILES):
            one_pass(acc_a, j, 1, q_a1, 0, 256)

        staged_b = placed("staged_b", [P, 256, PACK], BF16, 32)
        staged_c = placed("staged_c", [P, 256, PACK], BF16, 34)
        cast_q(on_scalar, staged_b, 0, raw_b0, 0, 128)
        act_a = placed("act_a", [P, SLOT_TILES, 256], F32, 5)
        activate(act_a, acc_a)
        cast_q(on_vector, staged_b, 128, raw_b1, 0, 128)
        q_b = quantize_q(staged_b, "b")
        acc_b = multiply_late("acc_b", 4, q_b)
        cast_q(on_vector, staged_c, 0, raw_c0, 0, 128)
        finish(placed("result_a0", [P, 1, 256], F32, 32), act_a, 0, 1, 0)
        cast_q(on_vector, staged_c, 128, raw_c1, 0, 128)
        finish(placed("result_a1", [P, 1, 256], F32, 16), act_a, 1, 2, 0)
        q_c = quantize_q(staged_c, "c")
        acc_c = multiply_late("acc_c", 0, q_c)
        finish(placed("result_a2", [P, 1, 256], F32, 18), act_a, 2, 3, 0)
        finish(placed("result_a3", [P, 1, 256], F32, 19), act_a, 3, 4, 0)

        act_b = placed("act_b", [P, SLOT_TILES, 128], F32, 36)
        activate(act_b, acc_b)
        finish(placed("result_b0", [P, 2, 128], F32, 34), act_b, 0, 2, 256)
        finish(placed("result_b2", [P, 2, 128], F32, 35), act_b, 2, 4, 256)
        act_c = placed("act_c", [P, SLOT_TILES, 128], F32, 38)
        activate(act_c, acc_c)
        finish(placed("result_c0", [P, 2, 128], F32, 40), act_c, 0, 2, 384)
        finish(placed("result_c2", [P, 1, 128], F32, 41), act_c, 2, 3, 384)
        finish(placed("result_c3", [P, 1, 128], F32, 42), act_c, 3, 4, 384)
